import numpy as np
import ml_dtypes


def mxq(x, axis, fmt="e4m3"):
    dtype, down = {"e4m3": (ml_dtypes.float8_e4m3fn, 7), "e5m2": (ml_dtypes.float8_e5m2, 14)}[fmt]
    v = np.moveaxis(np.asarray(x, np.float32).astype(ml_dtypes.bfloat16).astype(np.float64), axis, -1)
    blocks = v.reshape(v.shape[:-1] + (-1, 32))
    amax = np.abs(blocks).max(-1, keepdims=True)
    byte = np.maximum(np.where(amax > 0, np.frexp(amax)[1] - 1 + 127, 0) - down, 1)
    scale = np.exp2(byte - 127.0)
    codes = (blocks / scale).astype(np.float32).astype(dtype).astype(np.float64)
    return np.moveaxis((codes * scale).reshape(v.shape), -1, axis)


WIDE = False


def mx_kscale(k):
    if not WIDE:
        return np.ones(k)
    levels = np.array([10, -10, 5, -5, 0])
    if k % 512:
        return np.exp2(np.random.permutation(np.resize(levels, k // 32))).repeat(32)
    a = np.empty((k // 512, 16))
    for p in range(k // 512):
        a[p, :8] = np.random.permutation(np.resize(levels, 8))
        for g in range(8):
            far = levels[np.abs(levels - a[p, g]) >= 10]
            a[p, g + 8] = far[np.random.randint(len(far))]
    return np.exp2(a.ravel()).repeat(32)


def f64(x):
    return np.asarray(x).astype(np.float64)


def striped(idx):
    return np.tile(idx.reshape(-1, 16).T, (8, 1)).astype(np.uint16)


def unstriped(offs):
    return offs[:16].T.reshape(-1).astype(np.int64)


E2M1 = np.array([0.0, 0.5, 1.0, 1.5, 2.0, 3.0, 4.0, 6.0, -0.0, -0.5, -1.0, -1.5, -2.0, -3.0, -4.0, -6.0])


def pack_weight(w, fmt):
    k, n = w.shape
    w = f64(np.asarray(w, np.float32).astype(ml_dtypes.bfloat16)).reshape(k // 32, 32, n)
    amax = np.abs(w).max(1)
    if fmt == "e4m3":
        byte = np.frexp(amax)[1] - 1 + 127 - 7
    else:
        mant, ex = np.frexp(amax / 6.0)
        byte = np.where(mant > 0.5, ex, ex - 1) + 127
    byte = np.clip(np.where(amax > 0, byte, 1), 1, 254)
    scaled = (w * np.exp2(127.0 - byte)[:, None, :]).reshape(k, n).astype(np.float32)
    by_word = np.ascontiguousarray(scaled.reshape(k // 512, 128, 4, n).transpose(0, 1, 3, 2))
    if fmt == "e4m3":
        words = by_word.astype(ml_dtypes.float8_e4m3fn).view(np.uint8)
    else:
        c = by_word.astype(ml_dtypes.float4_e2m1fn).view(np.uint8) & 0xF
        words = (c[..., 0::2] | (c[..., 1::2] << 4)).reshape(k // 512, 128, 2 * n)
    return np.ascontiguousarray(words), np.ascontiguousarray(byte.astype(np.uint8).reshape(k // 512, 16, n))


def unpack_weight(words, scales, fmt):
    g, _, n = scales.shape
    words = np.ascontiguousarray(words).reshape(g, 128, n, -1)
    if fmt == "e4m3":
        vals = words.view(ml_dtypes.float8_e4m3fn).astype(np.float64)
    else:
        nib = np.empty((g, 128, n, 4), np.uint8)
        nib[..., 0::2] = words & 0xF
        nib[..., 1::2] = words >> 4
        vals = E2M1[nib]
    vals = vals * np.repeat(np.exp2(scales.astype(np.float64) - 127.0), 8, axis=1)[..., None]
    return vals.transpose(0, 1, 3, 2).reshape(g * 512, n)


def gelu(v):
    return 0.5 * v * (1.0 + np.tanh(np.sqrt(2.0 / np.pi) * (v + 0.044715 * v**3)))


def striped8(idx):
    return np.concatenate([v.reshape(-1, 16).T for v in idx]).astype(np.uint16)


def unstriped8(offs):
    return np.stack([offs[16 * g:16 * g + 16].T.reshape(-1) for g in range(8)]).astype(np.int64)


def runs(v, idx8):
    k = np.arange(v.shape[0])
    return v[k[:, None], idx8[k % 512 // 64]]


def bf(x):
    return np.asarray(x, np.float32).astype(ml_dtypes.bfloat16)


def planes(Y):
    n, m = Y.shape
    b = f64(bf(Y)).reshape(n // 32, 32, m)
    amax = np.abs(b).max(1)
    byte = np.clip(np.where(amax > 0, np.frexp(amax)[1] - 1 + 127 - 7, 1), 1, 254)
    codes = (b * np.exp2(127.0 - byte)[:, None, :]).reshape(n, m).astype(np.float32).astype(ml_dtypes.float8_e4m3fn).view(np.uint8)
    words = codes.reshape(n // 512, 128, 4, m).transpose(0, 1, 3, 2)
    return np.ascontiguousarray(words), np.ascontiguousarray(byte.astype(np.uint8).reshape(n // 512, 16, m))


K, H, N, T, S, P, D = 1024, 1024, 512, 2048, 1024, 512, 8


def setup_inputs():
    n = np.random.standard_normal
    s = mx_kscale(K)[:, None]
    u = mx_kscale(H)[:, None]
    tab_words, tab_scales = pack_weight(n((K, T)) * s, "e4m3")
    w1 = 0.9 * n((K, H)) / np.sqrt(K) / s
    gain = np.random.uniform(0.8, 2.2, H) * u[:, 0]
    w2_words, w2_scales = pack_weight(0.9 * n((H, H)) / np.sqrt(H) / u, "e2m1")
    tilt = 0.12 * n(H)
    mat = 5.0 * n((H, P)) * u
    size = np.exp(0.8 * n(N))
    w3 = n((H, N)) / np.sqrt(H) / u * size
    bo = 0.6 * n(N) * size
    idx8 = np.stack([np.random.permutation(S)[:P] for _ in range(D)])
    return {
        "tab_words": tab_words, "tab_scales": tab_scales,
        "offs": striped(np.random.permutation(T)[:S]),
        "w1": w1.astype(np.float32), "gain": gain.astype(np.float32),
        "w2_words": w2_words, "w2_scales": w2_scales,
        "offs2": striped8(idx8),
        "tilt": tilt.astype(np.float32), "mat": mat.astype(np.float32),
        "w3": w3.astype(np.float32), "bo": bo.astype(np.float32),
    }


def reference(tab_words, tab_scales, offs, w1, gain, w2_words, w2_scales, offs2, tilt, mat, w3, bo):
    v = unpack_weight(tab_words, tab_scales, "e4m3")[:, unstriped(offs)]
    x = mxq(f64(w1), 0, "e4m3").T @ v
    f = f64(gain)[:, None] * (0.5 * x * (1.0 + np.tanh(0.7978845608028654 * (x + 0.044715 * x * x * x))))
    w2 = unpack_weight(w2_words, w2_scales, "e2m1")
    h = np.maximum(x, w2.T @ mxq(f, 0, "e4m3"))
    top = h.max(axis=1)
    hp = runs(h, unstriped8(offs2))
    a = np.exp(hp - top[:, None])
    d = f64(mat) * (a + f64(tilt)[:, None])
    y = (mxq(f64(w3), 0, "e4m3").T @ mxq(d, 0, "e4m3")) + f64(bo)[:, None]
    words, scales = planes(y)
    return y, words, scales

@@ -1,0 +1,271 @@
+from contextlib import ExitStack
+
+import concourse.mybir as mybir
+
+F32 = mybir.dt.float32
+BF16 = mybir.dt.bfloat16
+I32 = mybir.dt.int32
+U32 = mybir.dt.uint32
+U16 = mybir.dt.uint16
+U8 = mybir.dt.uint8
+FP8X4 = mybir.dt.float8_e4m3fn_x4
+FP4X4 = mybir.dt.float4_e2m1fn_x4
+ACT = mybir.ActivationFunctionType
+ALU = mybir.AluOpType
+AX = mybir.AxisListType
+
+K, H, N, T, S, M = 1024, 1024, 512, 2048, 1024, 512
+P = 128
+PACK = 4
+PASS = P * PACK
+HALF = 512
+FLOPS = 2 * K * H * S + 2 * H * H * S + 2 * H * N * M
+
+
+def tile_list_tremolo_evenness_adviser_kernel(
+    tc, tab_words, tab_scales, offs, w1, gain, w2_words, w2_scales, offs2, tilt, mat, w3, bo, out_0, out_1, out_2
+):
+    nc = tc.nc
+    with ExitStack() as ctx:
+        keep = ctx.enter_context(tc.tile_pool(name="keep", bufs=1))
+        ring = ctx.enter_context(tc.tile_pool(name="ring", bufs=2))
+        psum = ctx.enter_context(tc.psum_pool(name="psum", bufs=1))
+
+        def held(shape, dtype, name):
+            return keep.tile(shape, dtype, name=name, align_bytes=64)
+
+        list1 = keep.tile([P, S // 16], U16, name="list1")
+        list2 = keep.tile([P, M // 16], U16, name="list2")
+        tab_w = [held([P, T], U32, f"tab_w{a}") for a in range(2)]
+        tab_s = held([P, T], U8, "tab_s")
+        w2_w_raw = held([P, 2, 2 * H], U8, "w2_w_raw")
+        w2_s_raw = held([P, 2, H], U8, "w2_s_raw")
+        w1_raw = [[held([P, PACK, PASS], F32, f"w1_raw{a}{b}") for b in range(2)] for a in range(2)]
+        w3_raw = [held([P, PACK, N], F32, f"w3_raw{b}") for b in range(2)]
+        mat_sb = [held([P, PACK, M], F32, f"mat{b}") for b in range(2)]
+        gain_sb = held([P, 2, PACK], F32, "gain_sb")
+        tilt_sb = held([P, 2, PACK], F32, "tilt_sb")
+        bo_sb = held([P, PACK], F32, "bo_sb")
+
+        nc.vector.memset(tab_s[:].bitcast(I32), 0)
+        nc.vector.memset(w2_s_raw[:].bitcast(I32), 0)
+
+        def load_w1(a, b):
+            rows = w1[PASS * a : PASS * (a + 1), PASS * b : PASS * (b + 1)]
+            nc.sync.dma_start(out=w1_raw[a][b][:], in_=rows.rearrange("(p j) c -> p j c", j=PACK))
+
+        def load_tab(a):
+            nc.sync.dma_start(
+                out=tab_w[a][:].bitcast(I32), in_=tab_words[a].rearrange("p t i -> p (t i)").bitcast(I32)
+            )
+
+        nc.sync.dma_start(list1[:], offs)
+        nc.sync.dma_start(out=w2_w_raw[:].bitcast(I32), in_=w2_words.bitcast(I32).rearrange("a p c -> p a c"))
+        load_tab(0)
+        load_w1(0, 0)
+        for q in range(4):
+            nc.scalar.dma_start(
+                out=tab_s[32 * q : 32 * q + 8, :].bitcast(I32), in_=tab_scales.bitcast(I32)[:, 4 * q : 4 * q + 4, :]
+            )
+        for q in range(4):
+            nc.scalar.dma_start(
+                out=w2_s_raw[32 * q : 32 * q + 4, :, :].bitcast(I32),
+                in_=w2_scales.bitcast(I32)[:, 4 * q : 4 * q + 4, :].rearrange("a r c -> r a c"),
+            )
+        nc.scalar.dma_start(out=gain_sb[:], in_=gain.rearrange("(b p i) -> p b i", b=2, i=PACK))
+        load_tab(1)
+        load_w1(1, 0)
+        load_w1(0, 1)
+        load_w1(1, 1)
+        nc.sync.dma_start(list2[:], offs2)
+        nc.sync.dma_start(out=tilt_sb[:], in_=tilt.rearrange("(b p i) -> p b i", b=2, i=PACK))
+        nc.sync.dma_start(out=bo_sb[:], in_=bo.rearrange("(p i) -> p i", i=PACK))
+        for b in range(2):
+            rows = w3[PASS * b : PASS * (b + 1), :]
+            nc.sync.dma_start(out=w3_raw[b][:], in_=rows.rearrange("(p j) c -> p j c", j=PACK))
+        for b in range(2):
+            rows = mat[PASS * b : PASS * (b + 1), :]
+            nc.sync.dma_start(out=mat_sb[b][:], in_=rows.rearrange("(p j) c -> p j c", j=PACK))
+
+        w2_w = held([P, 2, 2 * H], U8, "w2_w")
+        w2_s = held([P, 2, H], U8, "w2_s")
+        nc.scalar.copy(
+            out=w2_w[:].bitcast(U16).rearrange("p a (b i m) -> p (a b) m i", b=2, i=PACK),
+            in_=w2_w_raw[:].bitcast(U16).rearrange("p a (b m i) -> p (a b) m i", b=2, i=PACK),
+        )
+
+        v_w = [[held([P, HALF], U32, f"v_w{a}{c}") for c in range(2)] for a in range(2)]
+        v_s = [held([P, HALF], U8, f"v_s{c}") for c in range(2)]
+
+        def part(c):
+            return list1[:, 32 * c : 32 * (c + 1)]
+
+        for c in range(2):
+            nc.vector.tensor_copy(out=v_s[c][:], in_=tab_s[:].indirect(part(c)))
+        nc.vector.tensor_copy(
+            out=w2_s[:].rearrange("p a (b i m) -> p (a b) m i", b=2, i=PACK),
+            in_=w2_s_raw[:].rearrange("p a (b m i) -> p (a b) m i", b=2, i=PACK),
+        )
+
+        def deal(copy, raw, rounded, lo, hi):
+            copy(
+                out=rounded[:].rearrange("p t m j -> p m j t")[:, lo:hi],
+                in_=raw[:].rearrange("p j (m t) -> p m j t", t=PACK)[:, lo:hi],
+            )
+
+        def quantize(rounded_flat, name, width):
+            codes = held([P, width], U32, name + "_c")
+            scales = held([P, width], U8, name + "_s")
+            nc.vector.quantize_mx(out=codes[:].bitcast(FP8X4), scales=scales[:], in_=rounded_flat)
+            return codes, scales
+
+        w1_q = {}
+
+        def prepare_w1(a, b, scalar_share):
+            rounded = ring.tile([P, PACK, P, PACK], BF16, name="w_rounded", align_bytes=64)
+            if scalar_share > 0:
+                deal(nc.scalar.copy, w1_raw[a][b], rounded, 0, scalar_share)
+            if scalar_share < P:
+                deal(nc.vector.tensor_copy, w1_raw[a][b], rounded, scalar_share, P)
+            w1_q[a, b] = quantize(rounded[:].rearrange("p t m j -> p (t m j)"), f"w1q{a}{b}", PASS)
+
+        for c in range(2):
+            nc.vector.tensor_copy(out=v_w[0][c][:], in_=tab_w[0][:].indirect(part(c)))
+        for c in range(2):
+            nc.vector.tensor_copy(out=v_w[1][c][:], in_=tab_w[1][:].indirect(part(c)))
+        prepare_w1(0, 0, P)
+        prepare_w1(1, 0, 48)
+        prepare_w1(0, 1, 0)
+        prepare_w1(1, 1, 0)
+
+        h = [[held([P, S], F32, f"h{b}{i}") for i in range(PACK)] for b in range(2)]
+        part_top = [[held([P, 2], F32, f"ptop{b}{i}") for i in range(PACK)] for b in range(2)]
+        f_q = {}
+
+        def first_stage(b, c):
+            cols = slice(HALF * c, HALF * (c + 1))
+            g = ring.tile([P, PACK, HALF], F32, name="g", align_bytes=64)
+            for i in range(PACK):
+                acc = psum.tile([P, HALF], F32, name=f"xy{i}")
+                for a in range(2):
+                    codes, scales = w1_q[a, b]
+                    nc.tensor.matmul_mx(
+                        out=acc[:],
+                        lhsT=codes[:, P * i : P * (i + 1)].bitcast(FP8X4),
+                        lhsT_scale=scales[:, P * i : P * (i + 1)],
+                        rhs=v_w[a][c][:].bitcast(FP8X4),
+                        rhs_scale=v_s[c][4 * a : P, :],
+                        start=(a == 0),
+                        stop=(a == 1),
+                    )
+                nc.scalar.activation(out=g[:, i, :], in_=acc[:], func=ACT.Gelu_apprx_tanh)
+                nc.scalar.copy(out=h[b][i][:, cols], in_=acc[:])
+            f = ring.tile([P, HALF, PACK], BF16, name="woven", align_bytes=64)
+            nc.vector.tensor_tensor(
+                out=f[:].rearrange("p (c q) t -> p c t q", q=4),
+                in0=g[:].rearrange("p t (c q) -> p c t q", q=4),
+                in1=gain_sb[:, b, :].unsqueeze(1).unsqueeze(3).to_broadcast([P, HALF // 4, PACK, 4]),
+                op=ALU.mult,
+            )
+            f_q[b, c] = quantize(f[:].rearrange("p c t -> p (c t)"), f"fq{b}{c}", HALF)
+
+        def second_stage(b, i, c):
+            cols = slice(HALF * c, HALF * (c + 1))
+            acc = psum.tile([P, HALF], F32, name=f"z{i}")
+            first = PASS * b + P * i
+            for a in range(2):
+                codes, scales = f_q[a, c]
+                nc.tensor.matmul_mx(
+                    out=acc[:],
+                    lhsT=w2_w[:, a, 2 * first : 2 * (first + P)].bitcast(FP4X4),
+                    lhsT_scale=w2_s[:, a, first : first + P],
+                    rhs=codes[:].bitcast(FP8X4),
+                    rhs_scale=scales[:],
+                    start=(a == 0),
+                    stop=(a == 1),
+                )
+            nc.vector.tensor_tensor(out=h[b][i][:, cols], in0=acc[:], in1=h[b][i][:, cols], op=ALU.max)
+            nc.vector.tensor_reduce(out=part_top[b][i][:, c : c + 1], in_=h[b][i][:, cols], axis=AX.X, op=ALU.max)
+
+        w3_q = {}
+
+        def prepare_w3(b):
+            rounded = ring.tile([P, PACK, P, PACK], BF16, name="w_rounded", align_bytes=64)
+            deal(nc.scalar.copy, w3_raw[b], rounded, 0, P)
+            w3_q[b] = quantize(rounded[:].rearrange("p t m j -> p (t m j)"), f"w3q{b}", N)
+
+        first_stage(0, 0)
+        first_stage(1, 0)
+        first_stage(0, 1)
+        first_stage(1, 1)
+        for b in range(2):
+            for i in range(PACK):
+                second_stage(b, i, 0)
+        prepare_w3(0)
+        prepare_w3(1)
+
+        y_acc = [psum.tile([P, M], F32, name=f"xy{t}") for t in range(PACK)]
+        for b in range(2):
+            d_rows = ring.tile([P, PACK, M], BF16, name="d_rows", align_bytes=64)
+            for i in range(PACK):
+                second_stage(b, i, 1)
+                neg_top = held([P, 1], F32, f"ntop{b}{i}")
+                nc.vector.tensor_scalar(
+                    out=neg_top[:],
+                    in0=part_top[b][i][:, 0:1],
+                    scalar1=part_top[b][i][:, 1:2],
+                    scalar2=-1.0,
+                    op0=ALU.max,
+                    op1=ALU.mult,
+                )
+                look = ring.tile([P, M], F32, name="look", bufs=3, align_bytes=64)
+                nc.scalar.activation(out=look[:], in_=h[b][i][:].indirect(list2[:]), func=ACT.Exp, bias=neg_top[:])
+                nc.vector.scalar_tensor_tensor(
+                    out=d_rows[:, i, :],
+                    in0=look[:],
+                    scalar=tilt_sb[:, b, i : i + 1],
+                    in1=mat_sb[b][:, i, :],
+                    op0=ALU.add,
+                    op1=ALU.mult,
+                )
+            d = ring.tile([P, M, PACK], BF16, name="woven", align_bytes=64)
+            weave = nc.scalar.copy if b == 0 else nc.vector.tensor_copy
+            weave(
+                out=d[:].rearrange("p (c q) t -> p c t q", q=4),
+                in_=d_rows[:].rearrange("p t (c q) -> p c t q", q=4),
+            )
+            codes, scales = quantize(d[:].rearrange("p c t -> p (c t)"), f"dq{b}", M)
+            w_codes, w_scales = w3_q[b]
+            for t in range(PACK):
+                nc.tensor.matmul_mx(
+                    out=y_acc[t][:],
+                    lhsT=w_codes[:, P * t : P * (t + 1)].bitcast(FP8X4),
+                    lhsT_scale=w_scales[:, P * t : P * (t + 1)],
+                    rhs=codes[:].bitcast(FP8X4),
+                    rhs_scale=scales[:],
+                    start=(b == 0),
+                    stop=(b == 1),
+                )
+
+        y = held([P, PACK, M], F32, "y")
+        y_rows = out_0.rearrange("(p t) m -> p t m", t=PACK)
+        for t in range(PACK):
+            if t % 2 == 0:
+                nc.scalar.activation(out=y[:, t, :], in_=y_acc[t][:], func=ACT.Identity, bias=bo_sb[:, t : t + 1])
+            else:
+                nc.vector.tensor_scalar(
+                    out=y[:, t, :], in0=y_acc[t][:], scalar1=bo_sb[:, t : t + 1], scalar2=None, op0=ALU.add
+                )
+            nc.sync.dma_start(out=y_rows[:, t, :], in_=y[:, t, :])
+        y_woven = ring.tile([P, M, PACK], BF16, name="woven", align_bytes=64)
+        nc.vector.tensor_copy(
+            out=y_woven[:].rearrange("p (c q) t -> p c t q", q=4),
+            in_=y[:].rearrange("p t (c q) -> p c t q", q=4),
+        )
+        y_codes, y_scales = quantize(y_woven[:].rearrange("p c t -> p (c t)"), "yq", M)
+        nc.sync.dma_start(out=out_1[0].rearrange("p m t -> p (m t)").bitcast(I32), in_=y_codes[:].bitcast(I32))
+        for q in range(4):
+            queue = nc.scalar if q % 2 == 0 else nc.sync
+            queue.dma_start(
+                out=out_2[0].bitcast(I32)[4 * q : 4 * q + 4, :], in_=y_scales[32 * q : 32 * q + 4, :].bitcast(I32)
+            )

@@ -40,9 +40,9 @@ def tile_list_tremolo_evenness_adviser_kernel(
         tab_s = held([P, T], U8, "tab_s")
         w2_w_raw = held([P, 2, 2 * H], U8, "w2_w_raw")
         w2_s_raw = held([P, 2, H], U8, "w2_s_raw")
-        w1_raw = [[held([P, PACK, PASS], F32, f"w1_raw{a}{b}") for b in range(2)] for a in range(2)]
-        w3_raw = [held([P, PACK, N], F32, f"w3_raw{b}") for b in range(2)]
-        mat_sb = [held([P, PACK, M], F32, f"mat{b}") for b in range(2)]
+        staged = [ring.tile([P, PACK, PASS], F32, name="staged", bufs=6, align_bytes=64) for n in range(6)]
+        w1_raw = [[staged[0], staged[2]], [staged[1], staged[3]]]
+        w3_raw = staged[4:6]
         gain_sb = held([P, 2, PACK], F32, "gain_sb")
         tilt_sb = held([P, 2, PACK], F32, "tilt_sb")
         bo_sb = held([P, PACK], F32, "bo_sb")
@@ -61,20 +61,20 @@ def tile_list_tremolo_evenness_adviser_kernel(
 
         nc.sync.dma_start(list1[:], offs)
         nc.sync.dma_start(out=w2_w_raw[:].bitcast(I32), in_=w2_words.bitcast(I32).rearrange("a p c -> p a c"))
+        for q in range(4):
+            nc.sync.dma_start(
+                out=tab_s[32 * q : 32 * q + 8, :].bitcast(I32), in_=tab_scales.bitcast(I32)[:, 4 * q : 4 * q + 4, :]
+            )
         load_tab(0)
         load_w1(0, 0)
         for q in range(4):
-            nc.scalar.dma_start(
-                out=tab_s[32 * q : 32 * q + 8, :].bitcast(I32), in_=tab_scales.bitcast(I32)[:, 4 * q : 4 * q + 4, :]
-            )
-        for q in range(4):
-            nc.scalar.dma_start(
+            nc.sync.dma_start(
                 out=w2_s_raw[32 * q : 32 * q + 4, :, :].bitcast(I32),
                 in_=w2_scales.bitcast(I32)[:, 4 * q : 4 * q + 4, :].rearrange("a r c -> r a c"),
             )
-        nc.scalar.dma_start(out=gain_sb[:], in_=gain.rearrange("(b p i) -> p b i", b=2, i=PACK))
-        load_tab(1)
         load_w1(1, 0)
+        load_tab(1)
+        nc.sync.dma_start(out=gain_sb[:], in_=gain.rearrange("(b p i) -> p b i", b=2, i=PACK))
         load_w1(0, 1)
         load_w1(1, 1)
         nc.sync.dma_start(list2[:], offs2)
@@ -83,9 +83,6 @@ def tile_list_tremolo_evenness_adviser_kernel(
         for b in range(2):
             rows = w3[PASS * b : PASS * (b + 1), :]
             nc.sync.dma_start(out=w3_raw[b][:], in_=rows.rearrange("(p j) c -> p j c", j=PACK))
-        for b in range(2):
-            rows = mat[PASS * b : PASS * (b + 1), :]
-            nc.sync.dma_start(out=mat_sb[b][:], in_=rows.rearrange("(p j) c -> p j c", j=PACK))
 
         w2_w = held([P, 2, 2 * H], U8, "w2_w")
         w2_s = held([P, 2, H], U8, "w2_s")
@@ -122,7 +119,7 @@ def tile_list_tremolo_evenness_adviser_kernel(
         w1_q = {}
 
         def prepare_w1(a, b, scalar_share):
-            rounded = ring.tile([P, PACK, P, PACK], BF16, name="w_rounded", align_bytes=64)
+            rounded = held([P, PACK, P, PACK], BF16, f"bf16_{a}")
             if scalar_share > 0:
                 deal(nc.scalar.copy, w1_raw[a][b], rounded, 0, scalar_share)
             if scalar_share < P:
@@ -131,22 +128,36 @@ def tile_list_tremolo_evenness_adviser_kernel(
 
         for c in range(2):
             nc.vector.tensor_copy(out=v_w[0][c][:], in_=tab_w[0][:].indirect(part(c)))
+        prepare_w1(0, 0, P)
+        prepare_w1(1, 0, 96)
         for c in range(2):
             nc.vector.tensor_copy(out=v_w[1][c][:], in_=tab_w[1][:].indirect(part(c)))
-        prepare_w1(0, 0, P)
-        prepare_w1(1, 0, 48)
         prepare_w1(0, 1, 0)
         prepare_w1(1, 1, 0)
 
+        mat_sb = [ring.tile([P, PACK, M], F32, name="staged", bufs=6, align_bytes=64) for b in range(2)]
+        for b in range(2):
+            rows = mat[PASS * b : PASS * (b + 1), :]
+            nc.sync.dma_start(out=mat_sb[b][:], in_=rows.rearrange("(p j) c -> p j c", j=PACK))
         h = [[held([P, S], F32, f"h{b}{i}") for i in range(PACK)] for b in range(2)]
         part_top = [[held([P, 2], F32, f"ptop{b}{i}") for i in range(PACK)] for b in range(2)]
         f_q = {}
 
-        def first_stage(b, c):
-            cols = slice(HALF * c, HALF * (c + 1))
+        x_acc = {}
+
+        def weave(copy, rows, width):
+            woven = ring.tile([P, width, PACK], BF16, name="woven", bufs=3, align_bytes=64)
+            copy(
+                out=woven[:].rearrange("p (c q) t -> p c t q", q=4),
+                in_=rows.rearrange("p t (c q) -> p c t q", q=4),
+            )
+            return woven[:].rearrange("p c t -> p (c t)")
+
+        def first_stage(b, c, banks, how):
             g = ring.tile([P, PACK, HALF], F32, name="g", align_bytes=64)
             for i in range(PACK):
-                acc = psum.tile([P, HALF], F32, name=f"xy{i}")
+                acc = psum.tile([P, HALF], F32, name=f"{banks}{i}")
+                x_acc[b, i, c] = acc
                 for a in range(2):
                     codes, scales = w1_q[a, b]
                     nc.tensor.matmul_mx(
@@ -159,19 +170,43 @@ def tile_list_tremolo_evenness_adviser_kernel(
                         stop=(a == 1),
                     )
                 nc.scalar.activation(out=g[:, i, :], in_=acc[:], func=ACT.Gelu_apprx_tanh)
-                nc.scalar.copy(out=h[b][i][:, cols], in_=acc[:])
-            f = ring.tile([P, HALF, PACK], BF16, name="woven", align_bytes=64)
-            nc.vector.tensor_tensor(
-                out=f[:].rearrange("p (c q) t -> p c t q", q=4),
-                in0=g[:].rearrange("p t (c q) -> p c t q", q=4),
-                in1=gain_sb[:, b, :].unsqueeze(1).unsqueeze(3).to_broadcast([P, HALF // 4, PACK, 4]),
-                op=ALU.mult,
-            )
-            f_q[b, c] = quantize(f[:].rearrange("p c t -> p (c t)"), f"fq{b}{c}", HALF)
+            if how == "s" or how == "h":
+                f_rows = ring.tile([P, PACK, HALF], BF16, name="d_rows", bufs=3, align_bytes=64)
+                for i in range(PACK):
+                    nc.scalar.activation(out=f_rows[:, i, :], in_=g[:, i, :], func=ACT.Copy, scale=gain_sb[:, b, i : i + 1])
+                flat = weave(nc.scalar.copy if how == "s" else nc.vector.tensor_copy, f_rows[:], HALF)
+            else:
+                if (b, c) == (0, 0):
+                    f = held([P, HALF, PACK], BF16, "bf16_1")
+                else:
+                    f = ring.tile([P, HALF, PACK], BF16, name="woven", bufs=3, align_bytes=64)
+                flat = f[:].rearrange("p c t -> p (c t)")
+                if how == "g":
+                    width = HALF // 4
+                    for piece in range(4):
+                        cols = slice(width * piece, width * (piece + 1))
+                        nc.gpsimd.tensor_tensor(
+                            out=f[:, cols, :],
+                            in0=g[:].rearrange("p t c -> p c t")[:, cols, :],
+                            in1=gain_sb[:, b, :].unsqueeze(1).to_broadcast([P, width, PACK]),
+                            op=ALU.mult,
+                        )
+                else:
+                    nc.vector.tensor_tensor(
+                        out=f[:].rearrange("p (c q) t -> p c t q", q=4),
+                        in0=g[:].rearrange("p t (c q) -> p c t q", q=4),
+                        in1=gain_sb[:, b, :].unsqueeze(1).unsqueeze(3).to_broadcast([P, HALF // 4, PACK, 4]),
+                        op=ALU.mult,
+                    )
+            f_q[b, c] = quantize(flat, f"fq{b}{c}", HALF)
+
+        def keep_x(b, c, copy):
+            for i in range(PACK):
+                copy(out=h[b][i][:, HALF * c : HALF * (c + 1)], in_=x_acc[b, i, c][:])
 
         def second_stage(b, i, c):
             cols = slice(HALF * c, HALF * (c + 1))
-            acc = psum.tile([P, HALF], F32, name=f"z{i}")
+            acc = psum.tile([P, HALF], F32, name=f"low{2 * c + i % 2}")
             first = PASS * b + P * i
             for a in range(2):
                 codes, scales = f_q[a, c]
@@ -185,85 +220,115 @@ def tile_list_tremolo_evenness_adviser_kernel(
                     stop=(a == 1),
                 )
             nc.vector.tensor_tensor(out=h[b][i][:, cols], in0=acc[:], in1=h[b][i][:, cols], op=ALU.max)
-            nc.vector.tensor_reduce(out=part_top[b][i][:, c : c + 1], in_=h[b][i][:, cols], axis=AX.X, op=ALU.max)
 
         w3_q = {}
 
         def prepare_w3(b):
-            rounded = ring.tile([P, PACK, P, PACK], BF16, name="w_rounded", align_bytes=64)
-            deal(nc.scalar.copy, w3_raw[b], rounded, 0, P)
+            rounded = held([P, PACK, P, PACK], BF16, f"bf16_{b}")
+            deal(nc.scalar.copy, w3_raw[b], rounded, 0, 128)
             w3_q[b] = quantize(rounded[:].rearrange("p t m j -> p (t m j)"), f"w3q{b}", N)
 
-        first_stage(0, 0)
-        first_stage(1, 0)
-        first_stage(0, 1)
-        first_stage(1, 1)
-        for b in range(2):
-            for i in range(PACK):
-                second_stage(b, i, 0)
-        prepare_w3(0)
-        prepare_w3(1)
+        first_stage(0, 0, "low", "v")
+        first_stage(1, 0, "high", "v")
+        keep_x(0, 0, nc.scalar.copy)
+        keep_x(1, 0, nc.scalar.copy)
+        first_stage(0, 1, "high", "v")
+        keep_x(0, 1, nc.scalar.copy)
+        first_stage(1, 1, "high", "v")
+        keep_x(1, 1, nc.scalar.copy)
 
-        y_acc = [psum.tile([P, M], F32, name=f"xy{t}") for t in range(PACK)]
-        for b in range(2):
-            d_rows = ring.tile([P, PACK, M], BF16, name="d_rows", align_bytes=64)
-            for i in range(PACK):
-                second_stage(b, i, 1)
-                neg_top = held([P, 1], F32, f"ntop{b}{i}")
-                nc.vector.tensor_scalar(
-                    out=neg_top[:],
-                    in0=part_top[b][i][:, 0:1],
-                    scalar1=part_top[b][i][:, 1:2],
-                    scalar2=-1.0,
-                    op0=ALU.max,
-                    op1=ALU.mult,
-                )
-                look = ring.tile([P, M], F32, name="look", bufs=3, align_bytes=64)
-                nc.scalar.activation(out=look[:], in_=h[b][i][:].indirect(list2[:]), func=ACT.Exp, bias=neg_top[:])
-                nc.vector.scalar_tensor_tensor(
-                    out=d_rows[:, i, :],
-                    in0=look[:],
-                    scalar=tilt_sb[:, b, i : i + 1],
-                    in1=mat_sb[b][:, i, :],
-                    op0=ALU.add,
-                    op1=ALU.mult,
-                )
-            d = ring.tile([P, M, PACK], BF16, name="woven", align_bytes=64)
-            weave = nc.scalar.copy if b == 0 else nc.vector.tensor_copy
-            weave(
-                out=d[:].rearrange("p (c q) t -> p c t q", q=4),
-                in_=d_rows[:].rearrange("p t (c q) -> p c t q", q=4),
+        neg_top = {}
+        early = []
+
+        def close_rows(b, i):
+            neg_top[b, i] = held([P, 1], F32, f"ntop{b}{i}")
+            second_stage(b, i, 0)
+            if PACK * b + i in early:
+                nc.vector.tensor_reduce(out=part_top[b][i][:, 0:1], in_=h[b][i][:, 0:HALF], axis=AX.X, op=ALU.max)
+            second_stage(b, i, 1)
+            if PACK * b + i in early:
+                nc.vector.tensor_reduce(out=part_top[b][i][:, 1:2], in_=h[b][i][:, HALF:S], axis=AX.X, op=ALU.max)
+                nc.vector.tensor_reduce(out=neg_top[b, i][:], in_=part_top[b][i][:], axis=AX.X, op=ALU.max, negate=True)
+            else:
+                nc.vector.tensor_reduce(out=neg_top[b, i][:], in_=h[b][i][:], axis=AX.X, op=ALU.max, negate=True)
+
+        def look(b, i, lo, hi):
+            seen = held([P, hi - lo], F32, f"look{b}{i}{lo}")
+            picks = list2[:, lo // 16 : hi // 16]
+            nc.scalar.activation(out=seen[:], in_=h[b][i][:].indirect(picks), func=ACT.Exp, bias=neg_top[b, i][:])
+            return seen
+
+        def weigh(seen, b, i, lo, hi, d_rows):
+            nc.vector.scalar_tensor_tensor(
+                out=d_rows[:, i, :],
+                in0=seen[:],
+                scalar=tilt_sb[:, b, i : i + 1],
+                in1=mat_sb[b][:, i, lo:hi],
+                op0=ALU.add,
+                op1=ALU.mult,
             )
-            codes, scales = quantize(d[:].rearrange("p c t -> p (c t)"), f"dq{b}", M)
+
+        MH = M // 2
+        y_acc = [[psum.tile([P, 2, MH], F32, name=f"high{2 * u + s}") for s in range(2)] for u in range(2)]
+
+        def third_stage(b, u, codes, scales):
             w_codes, w_scales = w3_q[b]
             for t in range(PACK):
                 nc.tensor.matmul_mx(
-                    out=y_acc[t][:],
+                    out=y_acc[u][t // 2][:, t % 2, :],
                     lhsT=w_codes[:, P * t : P * (t + 1)].bitcast(FP8X4),
                     lhsT_scale=w_scales[:, P * t : P * (t + 1)],
-                    rhs=codes[:].bitcast(FP8X4),
-                    rhs_scale=scales[:],
-                    start=(b == 0),
-                    stop=(b == 1),
+                    rhs=codes.bitcast(FP8X4),
+                    rhs_scale=scales,
+                    start=(b == 0 and t % 2 == 0),
+                    stop=(b == 1 and t % 2 == 1),
                 )
 
-        y = held([P, PACK, M], F32, "y")
+        d_rows = ring.tile([P, PACK, M], BF16, name="d_rows", bufs=3, align_bytes=64)
+        seen0 = []
+        for i in range(PACK):
+            close_rows(0, i)
+            seen0.append(look(0, i, 0, M))
+        prepare_w3(0)
+        prepare_w3(1)
+
+        for i in range(PACK):
+            close_rows(1, i)
+            weigh(seen0[i], 0, i, 0, M, d_rows)
+
+
+        codes, scales = quantize(weave(nc.scalar.copy, d_rows[:], M), "dq0", M)
+        for u in range(2):
+            third_stage(0, u, codes[:, MH * u : MH * (u + 1)], scales[:, MH * u : MH * (u + 1)])
+
         y_rows = out_0.rearrange("(p t) m -> p t m", t=PACK)
-        for t in range(PACK):
-            if t % 2 == 0:
-                nc.scalar.activation(out=y[:, t, :], in_=y_acc[t][:], func=ACT.Identity, bias=bo_sb[:, t : t + 1])
-            else:
-                nc.vector.tensor_scalar(
-                    out=y[:, t, :], in0=y_acc[t][:], scalar1=bo_sb[:, t : t + 1], scalar2=None, op0=ALU.add
+        y_codes = held([P, M], U32, "y_codes")
+        y_scales = held([P, M], U8, "y_scales")
+        y_words = out_1[0].rearrange("p m t -> p (m t)").bitcast(I32)
+        for u in range(2):
+            d_rows = ring.tile([P, PACK, MH], BF16, name="d_rows", bufs=3, align_bytes=64)
+            for i in range(PACK):
+                weigh(look(1, i, MH * u, MH * (u + 1)), 1, i, MH * u, MH * (u + 1), d_rows)
+            codes, scales = quantize(weave([nc.vector.tensor_copy,nc.vector.tensor_copy][u], d_rows[:], MH), f"dq1{u}", MH)
+            third_stage(1, u, codes[:], scales[:])
+        for u in range(2):
+            cols = slice(MH * u, MH * (u + 1))
+            y = held([P, PACK, MH], F32, f"y{u}")
+            for t in range(2):
+                nc.scalar.activation(
+                    out=y[:, t, :], in_=y_acc[u][t // 2][:, t % 2, :], func=ACT.Identity, bias=bo_sb[:, t : t + 1]
                 )
-            nc.sync.dma_start(out=y_rows[:, t, :], in_=y[:, t, :])
-        y_woven = ring.tile([P, M, PACK], BF16, name="woven", align_bytes=64)
-        nc.vector.tensor_copy(
-            out=y_woven[:].rearrange("p (c q) t -> p c t q", q=4),
-            in_=y[:].rearrange("p t (c q) -> p c t q", q=4),
-        )
-        y_codes, y_scales = quantize(y_woven[:].rearrange("p c t -> p (c t)"), "yq", M)
-        nc.sync.dma_start(out=out_1[0].rearrange("p m t -> p (m t)").bitcast(I32), in_=y_codes[:].bitcast(I32))
+            nc.vector.tensor_tensor(
+                out=y[:, 2:4, :],
+                in0=y_acc[u][1][:],
+                in1=bo_sb[:, 2:4].unsqueeze(2).to_broadcast([P, 2, MH]),
+                op=ALU.add,
+            )
+            nc.sync.dma_start(out=y_rows[:, :, cols], in_=y[:])
+            nc.vector.quantize_mx(
+                out=y_codes[:, cols].bitcast(FP8X4), scales=y_scales[:, cols], in_=weave([nc.vector.tensor_copy,nc.vector.tensor_copy][u], y[:], MH)
+            )
+            nc.sync.dma_start(out=y_words[:, cols], in_=y_codes[:, cols].bitcast(I32))
         for q in range(4):
             queue = nc.scalar if q % 2 == 0 else nc.sync
             queue.dma_start(

@@ -74,9 +74,9 @@ def tile_list_tremolo_evenness_adviser_kernel(
             )
         load_w1(1, 0)
         load_tab(1)
-        nc.sync.dma_start(out=gain_sb[:], in_=gain.rearrange("(b p i) -> p b i", b=2, i=PACK))
         load_w1(0, 1)
         load_w1(1, 1)
+        nc.sync.dma_start(out=gain_sb[:], in_=gain.rearrange("(b p i) -> p b i", b=2, i=PACK))
         nc.sync.dma_start(list2[:], offs2)
         nc.sync.dma_start(out=tilt_sb[:], in_=tilt.rearrange("(b p i) -> p b i", b=2, i=PACK))
         nc.sync.dma_start(out=bo_sb[:], in_=bo.rearrange("(p i) -> p i", i=PACK))
@@ -153,56 +153,48 @@ def tile_list_tremolo_evenness_adviser_kernel(
             )
             return woven[:].rearrange("p c t -> p (c t)")
 
-        def first_stage(b, c, banks, how):
-            g = ring.tile([P, PACK, HALF], F32, name="g", align_bytes=64)
-            for i in range(PACK):
-                acc = psum.tile([P, HALF], F32, name=f"{banks}{i}")
-                x_acc[b, i, c] = acc
-                for a in range(2):
-                    codes, scales = w1_q[a, b]
-                    nc.tensor.matmul_mx(
-                        out=acc[:],
-                        lhsT=codes[:, P * i : P * (i + 1)].bitcast(FP8X4),
-                        lhsT_scale=scales[:, P * i : P * (i + 1)],
-                        rhs=v_w[a][c][:].bitcast(FP8X4),
-                        rhs_scale=v_s[c][4 * a : P, :],
-                        start=(a == 0),
-                        stop=(a == 1),
-                    )
-                nc.scalar.activation(out=g[:, i, :], in_=acc[:], func=ACT.Gelu_apprx_tanh)
-            if how == "s" or how == "h":
-                f_rows = ring.tile([P, PACK, HALF], BF16, name="d_rows", bufs=3, align_bytes=64)
-                for i in range(PACK):
-                    nc.scalar.activation(out=f_rows[:, i, :], in_=g[:, i, :], func=ACT.Copy, scale=gain_sb[:, b, i : i + 1])
-                flat = weave(nc.scalar.copy if how == "s" else nc.vector.tensor_copy, f_rows[:], HALF)
-            else:
-                if (b, c) == (0, 0):
-                    f = held([P, HALF, PACK], BF16, "bf16_1")
-                else:
-                    f = ring.tile([P, HALF, PACK], BF16, name="woven", bufs=3, align_bytes=64)
-                flat = f[:].rearrange("p c t -> p (c t)")
-                if how == "g":
-                    width = HALF // 4
-                    for piece in range(4):
-                        cols = slice(width * piece, width * (piece + 1))
-                        nc.gpsimd.tensor_tensor(
-                            out=f[:, cols, :],
-                            in0=g[:].rearrange("p t c -> p c t")[:, cols, :],
-                            in1=gain_sb[:, b, :].unsqueeze(1).to_broadcast([P, width, PACK]),
-                            op=ALU.mult,
-                        )
-                else:
-                    nc.vector.tensor_tensor(
-                        out=f[:].rearrange("p (c q) t -> p c t q", q=4),
-                        in0=g[:].rearrange("p t (c q) -> p c t q", q=4),
-                        in1=gain_sb[:, b, :].unsqueeze(1).unsqueeze(3).to_broadcast([P, HALF // 4, PACK, 4]),
-                        op=ALU.mult,
-                    )
-            f_q[b, c] = quantize(flat, f"fq{b}{c}", HALF)
+        CH = 128
+        x_kept = {}
 
-        def keep_x(b, c, copy):
-            for i in range(PACK):
-                copy(out=h[b][i][:, HALF * c : HALF * (c + 1)], in_=x_acc[b, i, c][:])
+        def first_stage(b, c, banks, on_gpsimd, pieces, f, kept, vector_copies):
+            g = ring.tile([P, HALF, PACK], F32, name="g", align_bytes=64)
+            x_kept[b, c] = kept
+            accs = []
+            for n in range(HALF // CH):
+                acc = psum.tile([P, PACK, CH], F32, name=f"{banks}{n}")
+                accs.append(acc)
+                cols = slice(CH * n, CH * (n + 1))
+                for i in range(PACK):
+                    for a in range(2):
+                        codes, scales = w1_q[a, b]
+                        nc.tensor.matmul_mx(
+                            out=acc[:, i, :],
+                            lhsT=codes[:, P * i : P * (i + 1)].bitcast(FP8X4),
+                            lhsT_scale=scales[:, P * i : P * (i + 1)],
+                            rhs=v_w[a][c][:, cols].bitcast(FP8X4),
+                            rhs_scale=v_s[c][4 * a : P, cols],
+                            start=(a == 0),
+                            stop=(a == 1),
+                        )
+                nc.scalar.activation(out=g[:, cols, :], in_=acc[:].rearrange("p i j -> p j i"), func=ACT.Gelu_apprx_tanh)
+            engine = nc.gpsimd if on_gpsimd else nc.vector
+            width = HALF // pieces
+            for piece in range(pieces):
+                cols = slice(width * piece, width * (piece + 1))
+                engine.tensor_tensor(
+                    out=f[:, cols, :],
+                    in0=g[:, cols, :],
+                    in1=gain_sb[:, b, :].unsqueeze(1).to_broadcast([P, width, PACK]),
+                    op=ALU.mult,
+                )
+            f_q[b, c] = quantize(f[:].rearrange("p c t -> p (c t)"), f"fq{b}{c}", HALF)
+            x_acc[b, c] = (accs, vector_copies)
+
+        def keep_x(b, c):
+            accs, vector_copies = x_acc[b, c]
+            for n in range(HALF // CH):
+                copy = nc.vector.tensor_copy if n in vector_copies else nc.scalar.copy
+                copy(out=x_kept[b, c][:, n], in_=accs[n][:])
 
         def second_stage(b, i, c):
             cols = slice(HALF * c, HALF * (c + 1))
@@ -219,7 +211,12 @@ def tile_list_tremolo_evenness_adviser_kernel(
                     start=(a == 0),
                     stop=(a == 1),
                 )
-            nc.vector.tensor_tensor(out=h[b][i][:, cols], in0=acc[:], in1=h[b][i][:, cols], op=ALU.max)
+            nc.vector.tensor_tensor(
+                out=h[b][i][:, cols].rearrange("p (n j) -> p n j", j=CH),
+                in0=acc[:].rearrange("p (n j) -> p n j", j=CH),
+                in1=x_kept[b, c][:, :, i, :],
+                op=ALU.max,
+            )
 
         w3_q = {}
 
@@ -228,14 +225,20 @@ def tile_list_tremolo_evenness_adviser_kernel(
             deal(nc.scalar.copy, w3_raw[b], rounded, 0, 128)
             w3_q[b] = quantize(rounded[:].rearrange("p t m j -> p (t m j)"), f"w3q{b}", N)
 
-        first_stage(0, 0, "low", "v")
-        first_stage(1, 0, "high", "v")
-        keep_x(0, 0, nc.scalar.copy)
-        keep_x(1, 0, nc.scalar.copy)
-        first_stage(0, 1, "high", "v")
-        keep_x(0, 1, nc.scalar.copy)
-        first_stage(1, 1, "high", "v")
-        keep_x(1, 1, nc.scalar.copy)
+        def woven_tile():
+            return ring.tile([P, HALF, PACK], BF16, name="woven", bufs=3, align_bytes=64)
+
+        def staged_x():
+            return ring.tile([P, HALF // CH, PACK, CH], F32, name="staged", bufs=6, align_bytes=64)
+
+        first_stage(0, 0, "low", False, 1, held([P, HALF, PACK], BF16, "bf16_1"), held([P, HALF // CH, PACK, CH], F32, "tab_w0"), [])
+        first_stage(1, 0, "high", False, 1, woven_tile(), held([P, HALF // CH, PACK, CH], F32, "tab_w1"), [])
+        keep_x(0, 0)
+        keep_x(1, 0)
+        first_stage(0, 1, "high", False, 1, woven_tile(), staged_x(), [])
+        keep_x(0, 1)
+        first_stage(1, 1, "high", False, 1, woven_tile(), staged_x(), [])
+        keep_x(1, 1)
 
         neg_top = {}
         early = []

@@ -18,7 +18,16 @@ K, H, N, T, S, M = 1024, 1024, 512, 2048, 1024, 512
 P = 128
 PACK = 4
 PASS = P * PACK
-HALF = 512
+PASSES = 2
+STRIPE = 16
+QUADRANT = 32
+SCALE_ROWS = 4
+HALF = S // 2
+CHUNK = HALF // PACK
+M_HALF = M // 2
+LINE = 4
+SCALAR_SHARE = 96
+STAGED_BUFS = 6
 FLOPS = 2 * K * H * S + 2 * H * H * S + 2 * H * N * M
 
 
@@ -34,74 +43,83 @@ def tile_list_tremolo_evenness_adviser_kernel(
         def held(shape, dtype, name):
             return keep.tile(shape, dtype, name=name, align_bytes=64)
 
-        list1 = keep.tile([P, S // 16], U16, name="list1")
-        list2 = keep.tile([P, M // 16], U16, name="list2")
-        tab_w = [held([P, T], U32, f"tab_w{a}") for a in range(2)]
+        def staged(shape):
+            return ring.tile(shape, F32, name="staged", bufs=STAGED_BUFS, align_bytes=64)
+
+        def woven_tile(width):
+            return ring.tile([P, width, PACK], BF16, name="woven", bufs=3, align_bytes=64)
+
+        def load_rows(tile, rows):
+            nc.sync.dma_start(out=tile[:], in_=rows.rearrange("(p j) c -> p j c", j=PACK))
+
+        list1 = keep.tile([P, S // STRIPE], U16, name="list1")
+        list2 = keep.tile([P, M // STRIPE], U16, name="list2")
+        tab_w = [held([P, T], U32, f"big{a}") for a in range(PASSES)]
         tab_s = held([P, T], U8, "tab_s")
-        w2_w_raw = held([P, 2, 2 * H], U8, "w2_w_raw")
-        w2_s_raw = held([P, 2, H], U8, "w2_s_raw")
-        staged = [ring.tile([P, PACK, PASS], F32, name="staged", bufs=6, align_bytes=64) for n in range(6)]
-        w1_raw = [[staged[0], staged[2]], [staged[1], staged[3]]]
-        w3_raw = staged[4:6]
-        gain_sb = held([P, 2, PACK], F32, "gain_sb")
-        tilt_sb = held([P, 2, PACK], F32, "tilt_sb")
+        w2_w_raw = held([P, PASSES, 2 * H], U8, "w2_w_raw")
+        w2_s_raw = held([P, PASSES, H], U8, "w2_s_raw")
+        w1_raw = {(a, b): staged([P, PACK, PASS]) for b in range(PASSES) for a in range(PASSES)}
+        w3_raw = [staged([P, PACK, N]) for b in range(PASSES)]
+        gain_sb = held([P, PASSES, PACK], F32, "gain_sb")
+        tilt_sb = held([P, PASSES, PACK], F32, "tilt_sb")
         bo_sb = held([P, PACK], F32, "bo_sb")
 
         nc.vector.memset(tab_s[:].bitcast(I32), 0)
         nc.vector.memset(w2_s_raw[:].bitcast(I32), 0)
 
         def load_w1(a, b):
-            rows = w1[PASS * a : PASS * (a + 1), PASS * b : PASS * (b + 1)]
-            nc.sync.dma_start(out=w1_raw[a][b][:], in_=rows.rearrange("(p j) c -> p j c", j=PACK))
+            load_rows(w1_raw[a, b], w1[PASS * a : PASS * (a + 1), PASS * b : PASS * (b + 1)])
 
         def load_tab(a):
             nc.sync.dma_start(
                 out=tab_w[a][:].bitcast(I32), in_=tab_words[a].rearrange("p t i -> p (t i)").bitcast(I32)
             )
 
+        quadrants = range(P // QUADRANT)
         nc.sync.dma_start(list1[:], offs)
         nc.sync.dma_start(out=w2_w_raw[:].bitcast(I32), in_=w2_words.bitcast(I32).rearrange("a p c -> p a c"))
-        for q in range(4):
+        for q in quadrants:
             nc.sync.dma_start(
-                out=tab_s[32 * q : 32 * q + 8, :].bitcast(I32), in_=tab_scales.bitcast(I32)[:, 4 * q : 4 * q + 4, :]
+                out=tab_s[QUADRANT * q : QUADRANT * q + PASSES * SCALE_ROWS, :].bitcast(I32),
+                in_=tab_scales.bitcast(I32)[:, SCALE_ROWS * q : SCALE_ROWS * (q + 1), :],
             )
         load_tab(0)
         load_w1(0, 0)
-        for q in range(4):
+        for q in quadrants:
             nc.sync.dma_start(
-                out=w2_s_raw[32 * q : 32 * q + 4, :, :].bitcast(I32),
-                in_=w2_scales.bitcast(I32)[:, 4 * q : 4 * q + 4, :].rearrange("a r c -> r a c"),
+                out=w2_s_raw[QUADRANT * q : QUADRANT * q + SCALE_ROWS, :, :].bitcast(I32),
+                in_=w2_scales.bitcast(I32)[:, SCALE_ROWS * q : SCALE_ROWS * (q + 1), :].rearrange("a r c -> r a c"),
             )
         load_w1(1, 0)
         load_tab(1)
         load_w1(0, 1)
         load_w1(1, 1)
-        nc.sync.dma_start(out=gain_sb[:], in_=gain.rearrange("(b p i) -> p b i", b=2, i=PACK))
+        nc.sync.dma_start(out=gain_sb[:], in_=gain.rearrange("(b p i) -> p b i", b=PASSES, i=PACK))
         nc.sync.dma_start(list2[:], offs2)
-        nc.sync.dma_start(out=tilt_sb[:], in_=tilt.rearrange("(b p i) -> p b i", b=2, i=PACK))
+        nc.sync.dma_start(out=tilt_sb[:], in_=tilt.rearrange("(b p i) -> p b i", b=PASSES, i=PACK))
         nc.sync.dma_start(out=bo_sb[:], in_=bo.rearrange("(p i) -> p i", i=PACK))
-        for b in range(2):
-            rows = w3[PASS * b : PASS * (b + 1), :]
-            nc.sync.dma_start(out=w3_raw[b][:], in_=rows.rearrange("(p j) c -> p j c", j=PACK))
+        for b in range(PASSES):
+            load_rows(w3_raw[b], w3[PASS * b : PASS * (b + 1), :])
 
-        w2_w = held([P, 2, 2 * H], U8, "w2_w")
-        w2_s = held([P, 2, H], U8, "w2_s")
+        w2_w = held([P, PASSES, 2 * H], U8, "w2_w")
+        w2_s = held([P, PASSES, H], U8, "w2_s")
         nc.scalar.copy(
-            out=w2_w[:].bitcast(U16).rearrange("p a (b i m) -> p (a b) m i", b=2, i=PACK),
-            in_=w2_w_raw[:].bitcast(U16).rearrange("p a (b m i) -> p (a b) m i", b=2, i=PACK),
+            out=w2_w[:].bitcast(U16).rearrange("p a (b i m) -> p (a b) m i", b=PASSES, i=PACK),
+            in_=w2_w_raw[:].bitcast(U16).rearrange("p a (b m i) -> p (a b) m i", b=PASSES, i=PACK),
         )
 
-        v_w = [[held([P, HALF], U32, f"v_w{a}{c}") for c in range(2)] for a in range(2)]
+        v_w = [[held([P, HALF], U32, f"v_w{a}{c}") for c in range(2)] for a in range(PASSES)]
         v_s = [held([P, HALF], U8, f"v_s{c}") for c in range(2)]
 
-        def part(c):
-            return list1[:, 32 * c : 32 * (c + 1)]
+        def gather(out, window, c):
+            entries = list1[:, HALF // STRIPE * c : HALF // STRIPE * (c + 1)]
+            nc.vector.tensor_copy(out=out[:], in_=window[:].indirect(entries))
 
         for c in range(2):
-            nc.vector.tensor_copy(out=v_s[c][:], in_=tab_s[:].indirect(part(c)))
+            gather(v_s[c], tab_s, c)
         nc.vector.tensor_copy(
-            out=w2_s[:].rearrange("p a (b i m) -> p (a b) m i", b=2, i=PACK),
-            in_=w2_s_raw[:].rearrange("p a (b m i) -> p (a b) m i", b=2, i=PACK),
+            out=w2_s[:].rearrange("p a (b i m) -> p (a b) m i", b=PASSES, i=PACK),
+            in_=w2_s_raw[:].rearrange("p a (b m i) -> p (a b) m i", b=PASSES, i=PACK),
         )
 
         def deal(copy, raw, rounded, lo, hi):
@@ -110,97 +128,90 @@ def tile_list_tremolo_evenness_adviser_kernel(
                 in_=raw[:].rearrange("p j (m t) -> p m j t", t=PACK)[:, lo:hi],
             )
 
-        def quantize(rounded_flat, name, width):
+        def quantize(values, name, width):
             codes = held([P, width], U32, name + "_c")
             scales = held([P, width], U8, name + "_s")
-            nc.vector.quantize_mx(out=codes[:].bitcast(FP8X4), scales=scales[:], in_=rounded_flat)
+            nc.vector.quantize_mx(out=codes[:].bitcast(FP8X4), scales=scales[:], in_=values)
             return codes, scales
 
         w1_q = {}
 
-        def prepare_w1(a, b, scalar_share):
-            rounded = held([P, PACK, P, PACK], BF16, f"bf16_{a}")
-            if scalar_share > 0:
-                deal(nc.scalar.copy, w1_raw[a][b], rounded, 0, scalar_share)
-            if scalar_share < P:
-                deal(nc.vector.tensor_copy, w1_raw[a][b], rounded, scalar_share, P)
+        def prepare_w1(a, b, scalar_groups):
+            rounded = held([P, PACK, P, PACK], BF16, f"rounded{a}")
+            if scalar_groups > 0:
+                deal(nc.scalar.copy, w1_raw[a, b], rounded, 0, scalar_groups)
+            if scalar_groups < P:
+                deal(nc.vector.tensor_copy, w1_raw[a, b], rounded, scalar_groups, P)
             w1_q[a, b] = quantize(rounded[:].rearrange("p t m j -> p (t m j)"), f"w1q{a}{b}", PASS)
 
         for c in range(2):
-            nc.vector.tensor_copy(out=v_w[0][c][:], in_=tab_w[0][:].indirect(part(c)))
+            gather(v_w[0][c], tab_w[0], c)
         prepare_w1(0, 0, P)
-        prepare_w1(1, 0, 96)
+        prepare_w1(1, 0, SCALAR_SHARE)
         for c in range(2):
-            nc.vector.tensor_copy(out=v_w[1][c][:], in_=tab_w[1][:].indirect(part(c)))
+            gather(v_w[1][c], tab_w[1], c)
         prepare_w1(0, 1, 0)
         prepare_w1(1, 1, 0)
 
-        mat_sb = [ring.tile([P, PACK, M], F32, name="staged", bufs=6, align_bytes=64) for b in range(2)]
-        for b in range(2):
-            rows = mat[PASS * b : PASS * (b + 1), :]
-            nc.sync.dma_start(out=mat_sb[b][:], in_=rows.rearrange("(p j) c -> p j c", j=PACK))
-        h = [[held([P, S], F32, f"h{b}{i}") for i in range(PACK)] for b in range(2)]
-        part_top = [[held([P, 2], F32, f"ptop{b}{i}") for i in range(PACK)] for b in range(2)]
+        mat_sb = [staged([P, PACK, M]) for b in range(PASSES)]
+        for b in range(PASSES):
+            load_rows(mat_sb[b], mat[PASS * b : PASS * (b + 1), :])
+        h = [[held([P, S], F32, f"h{b}{i}") for i in range(PACK)] for b in range(PASSES)]
+        half_top = [[held([P, 2], F32, f"half_top{b}{i}") for i in range(PACK)] for b in range(PASSES)]
         f_q = {}
-
-        x_acc = {}
+        x_banks = {}
+        x_kept = {}
 
         def weave(copy, rows, width):
-            woven = ring.tile([P, width, PACK], BF16, name="woven", bufs=3, align_bytes=64)
+            woven = woven_tile(width)
             copy(
-                out=woven[:].rearrange("p (c q) t -> p c t q", q=4),
-                in_=rows.rearrange("p t (c q) -> p c t q", q=4),
+                out=woven[:].rearrange("p (c q) t -> p c t q", q=LINE),
+                in_=rows.rearrange("p t (c q) -> p c t q", q=LINE),
             )
             return woven[:].rearrange("p c t -> p (c t)")
 
-        CH = 128
-        x_kept = {}
-
-        def first_stage(b, c, banks, on_gpsimd, pieces, f, kept, vector_copies):
-            g = ring.tile([P, HALF, PACK], F32, name="g", align_bytes=64)
-            x_kept[b, c] = kept
-            accs = []
-            for n in range(HALF // CH):
-                acc = psum.tile([P, PACK, CH], F32, name=f"{banks}{n}")
-                accs.append(acc)
-                cols = slice(CH * n, CH * (n + 1))
+        def first_stage(b, c, banks, f, engine, pieces):
+            gelu = ring.tile([P, HALF, PACK], F32, name="gelu", align_bytes=64)
+            x_banks[b, c] = []
+            for n in range(HALF // CHUNK):
+                acc = psum.tile([P, PACK, CHUNK], F32, name=f"{banks}{n}")
+                x_banks[b, c].append(acc)
+                cols = slice(CHUNK * n, CHUNK * (n + 1))
                 for i in range(PACK):
-                    for a in range(2):
+                    for a in range(PASSES):
                         codes, scales = w1_q[a, b]
                         nc.tensor.matmul_mx(
                             out=acc[:, i, :],
                             lhsT=codes[:, P * i : P * (i + 1)].bitcast(FP8X4),
                             lhsT_scale=scales[:, P * i : P * (i + 1)],
                             rhs=v_w[a][c][:, cols].bitcast(FP8X4),
-                            rhs_scale=v_s[c][4 * a : P, cols],
+                            rhs_scale=v_s[c][SCALE_ROWS * a : P, cols],
                             start=(a == 0),
-                            stop=(a == 1),
+                            stop=(a == PASSES - 1),
                         )
-                nc.scalar.activation(out=g[:, cols, :], in_=acc[:].rearrange("p i j -> p j i"), func=ACT.Gelu_apprx_tanh)
-            engine = nc.gpsimd if on_gpsimd else nc.vector
+                nc.scalar.activation(
+                    out=gelu[:, cols, :], in_=acc[:].rearrange("p i j -> p j i"), func=ACT.Gelu_apprx_tanh
+                )
             width = HALF // pieces
             for piece in range(pieces):
                 cols = slice(width * piece, width * (piece + 1))
                 engine.tensor_tensor(
                     out=f[:, cols, :],
-                    in0=g[:, cols, :],
+                    in0=gelu[:, cols, :],
                     in1=gain_sb[:, b, :].unsqueeze(1).to_broadcast([P, width, PACK]),
                     op=ALU.mult,
                 )
-            f_q[b, c] = quantize(f[:].rearrange("p c t -> p (c t)"), f"fq{b}{c}", HALF)
-            x_acc[b, c] = (accs, vector_copies)
 
-        def keep_x(b, c):
-            accs, vector_copies = x_acc[b, c]
-            for n in range(HALF // CH):
-                copy = nc.vector.tensor_copy if n in vector_copies else nc.scalar.copy
-                copy(out=x_kept[b, c][:, n], in_=accs[n][:])
+        def keep_x(b, c, kept):
+            x_kept[b, c] = kept
+            for n in range(HALF // CHUNK):
+                nc.scalar.copy(out=kept[:, n], in_=x_banks[b, c][n][:])
 
         def second_stage(b, i, c):
             cols = slice(HALF * c, HALF * (c + 1))
             acc = psum.tile([P, HALF], F32, name=f"low{2 * c + i % 2}")
             first = PASS * b + P * i
-            for a in range(2):
+            for a in range(PASSES):
                 codes, scales = f_q[a, c]
                 nc.tensor.matmul_mx(
                     out=acc[:],
@@ -209,56 +220,57 @@ def tile_list_tremolo_evenness_adviser_kernel(
                     rhs=codes[:].bitcast(FP8X4),
                     rhs_scale=scales[:],
                     start=(a == 0),
-                    stop=(a == 1),
+                    stop=(a == PASSES - 1),
                 )
             nc.vector.tensor_tensor(
-                out=h[b][i][:, cols].rearrange("p (n j) -> p n j", j=CH),
-                in0=acc[:].rearrange("p (n j) -> p n j", j=CH),
+                out=h[b][i][:, cols].rearrange("p (n j) -> p n j", j=CHUNK),
+                in0=acc[:].rearrange("p (n j) -> p n j", j=CHUNK),
                 in1=x_kept[b, c][:, :, i, :],
                 op=ALU.max,
             )
+            nc.vector.tensor_reduce(out=half_top[b][i][:, c : c + 1], in_=h[b][i][:, cols], axis=AX.X, op=ALU.max)
 
         w3_q = {}
 
         def prepare_w3(b):
-            rounded = held([P, PACK, P, PACK], BF16, f"bf16_{b}")
-            deal(nc.scalar.copy, w3_raw[b], rounded, 0, 128)
+            rounded = held([P, PACK, P, PACK], BF16, f"rounded{b}")
+            deal(nc.scalar.copy, w3_raw[b], rounded, 0, P)
             w3_q[b] = quantize(rounded[:].rearrange("p t m j -> p (t m j)"), f"w3q{b}", N)
 
-        def woven_tile():
-            return ring.tile([P, HALF, PACK], BF16, name="woven", bufs=3, align_bytes=64)
-
-        def staged_x():
-            return ring.tile([P, HALF // CH, PACK, CH], F32, name="staged", bufs=6, align_bytes=64)
-
-        first_stage(0, 0, "low", False, 1, held([P, HALF, PACK], BF16, "bf16_1"), held([P, HALF // CH, PACK, CH], F32, "tab_w0"), [])
-        first_stage(1, 0, "high", False, 1, woven_tile(), held([P, HALF // CH, PACK, CH], F32, "tab_w1"), [])
-        keep_x(0, 0)
-        keep_x(1, 0)
-        first_stage(0, 1, "high", False, 1, woven_tile(), staged_x(), [])
-        keep_x(0, 1)
-        first_stage(1, 1, "high", False, 1, woven_tile(), staged_x(), [])
-        keep_x(1, 1)
+        x_shape = [P, HALF // CHUNK, PACK, CHUNK]
+        f_late = held([P, PASSES, HALF, PACK], BF16, "f_late")
+        x_early = []
+        for b in range(PASSES):
+            f = held([P, HALF, PACK], BF16, "rounded1") if b == 0 else woven_tile(HALF)
+            x_early.append(held(x_shape, F32, f"big{b}"))
+            first_stage(b, 0, ("low", "high")[b], f[:], nc.vector, 1)
+            f_q[b, 0] = quantize(f[:].rearrange("p c t -> p (c t)"), f"fq{b}0", HALF)
+        for b in range(PASSES):
+            keep_x(b, 0, x_early[b])
+        for b in range(PASSES):
+            kept = staged(x_shape)
+            first_stage(b, 1, "high", f_late[:, b], nc.gpsimd, HALF // CHUNK)
+            keep_x(b, 1, kept)
+        for b in range(PASSES):
+            for i in range(PACK):
+                second_stage(b, i, 0)
+        late_codes, late_scales = quantize(f_late[:].rearrange("p b c t -> p (b c t)"), "fq_late", PASSES * HALF)
+        for a in range(PASSES):
+            f_q[a, 1] = (late_codes[:, HALF * a : HALF * (a + 1)], late_scales[:, HALF * a : HALF * (a + 1)])
+        for b in range(PASSES):
+            prepare_w3(b)
 
         neg_top = {}
-        early = []
 
         def close_rows(b, i):
-            neg_top[b, i] = held([P, 1], F32, f"ntop{b}{i}")
-            second_stage(b, i, 0)
-            if PACK * b + i in early:
-                nc.vector.tensor_reduce(out=part_top[b][i][:, 0:1], in_=h[b][i][:, 0:HALF], axis=AX.X, op=ALU.max)
+            neg_top[b, i] = held([P, 1], F32, f"neg_top{b}{i}")
             second_stage(b, i, 1)
-            if PACK * b + i in early:
-                nc.vector.tensor_reduce(out=part_top[b][i][:, 1:2], in_=h[b][i][:, HALF:S], axis=AX.X, op=ALU.max)
-                nc.vector.tensor_reduce(out=neg_top[b, i][:], in_=part_top[b][i][:], axis=AX.X, op=ALU.max, negate=True)
-            else:
-                nc.vector.tensor_reduce(out=neg_top[b, i][:], in_=h[b][i][:], axis=AX.X, op=ALU.max, negate=True)
+            nc.vector.tensor_reduce(out=neg_top[b, i][:], in_=half_top[b][i][:], axis=AX.X, op=ALU.max, negate=True)
 
         def look(b, i, lo, hi):
-            seen = held([P, hi - lo], F32, f"look{b}{i}{lo}")
-            picks = list2[:, lo // 16 : hi // 16]
-            nc.scalar.activation(out=seen[:], in_=h[b][i][:].indirect(picks), func=ACT.Exp, bias=neg_top[b, i][:])
+            seen = held([P, hi - lo], F32, f"seen{b}{i}{lo}")
+            entries = list2[:, lo // STRIPE : hi // STRIPE]
+            nc.scalar.activation(out=seen[:], in_=h[b][i][:].indirect(entries), func=ACT.Exp, bias=neg_top[b, i][:])
             return seen
 
         def weigh(seen, b, i, lo, hi, d_rows):
@@ -271,8 +283,10 @@ def tile_list_tremolo_evenness_adviser_kernel(
                 op1=ALU.mult,
             )
 
-        MH = M // 2
-        y_acc = [[psum.tile([P, 2, MH], F32, name=f"high{2 * u + s}") for s in range(2)] for u in range(2)]
+        def d_tile(width):
+            return ring.tile([P, PACK, width], BF16, name="d_rows", bufs=3, align_bytes=64)
+
+        y_acc = [[psum.tile([P, 2, M_HALF], F32, name=f"high{2 * u + s}") for s in range(2)] for u in range(2)]
 
         def third_stage(b, u, codes, scales):
             w_codes, w_scales = w3_q[b]
@@ -284,56 +298,57 @@ def tile_list_tremolo_evenness_adviser_kernel(
                     rhs=codes.bitcast(FP8X4),
                     rhs_scale=scales,
                     start=(b == 0 and t % 2 == 0),
-                    stop=(b == 1 and t % 2 == 1),
+                    stop=(b == PASSES - 1 and t % 2 == 1),
                 )
 
-        d_rows = ring.tile([P, PACK, M], BF16, name="d_rows", bufs=3, align_bytes=64)
-        seen0 = []
+        d_first = d_tile(M)
+        seen_first = []
         for i in range(PACK):
             close_rows(0, i)
-            seen0.append(look(0, i, 0, M))
-        prepare_w3(0)
-        prepare_w3(1)
-
+            seen_first.append(look(0, i, 0, M))
         for i in range(PACK):
             close_rows(1, i)
-            weigh(seen0[i], 0, i, 0, M, d_rows)
-
-
-        codes, scales = quantize(weave(nc.scalar.copy, d_rows[:], M), "dq0", M)
+        for i in range(PACK):
+            weigh(seen_first[i], 0, i, 0, M, d_first)
+        d_codes, d_scales = quantize(weave(nc.scalar.copy, d_first[:], M), "dq0", M)
+        halves = [slice(M_HALF * u, M_HALF * (u + 1)) for u in range(2)]
         for u in range(2):
-            third_stage(0, u, codes[:, MH * u : MH * (u + 1)], scales[:, MH * u : MH * (u + 1)])
+            third_stage(0, u, d_codes[:, halves[u]], d_scales[:, halves[u]])
 
         y_rows = out_0.rearrange("(p t) m -> p t m", t=PACK)
         y_codes = held([P, M], U32, "y_codes")
         y_scales = held([P, M], U8, "y_scales")
         y_words = out_1[0].rearrange("p m t -> p (m t)").bitcast(I32)
         for u in range(2):
-            d_rows = ring.tile([P, PACK, MH], BF16, name="d_rows", bufs=3, align_bytes=64)
+            d_half = d_tile(M_HALF)
+            lo, hi = halves[u].start, halves[u].stop
             for i in range(PACK):
-                weigh(look(1, i, MH * u, MH * (u + 1)), 1, i, MH * u, MH * (u + 1), d_rows)
-            codes, scales = quantize(weave([nc.vector.tensor_copy,nc.vector.tensor_copy][u], d_rows[:], MH), f"dq1{u}", MH)
-            third_stage(1, u, codes[:], scales[:])
+                weigh(look(1, i, lo, hi), 1, i, lo, hi, d_half)
+            half_codes, half_scales = quantize(weave(nc.vector.tensor_copy, d_half[:], M_HALF), f"dq1{u}", M_HALF)
+            third_stage(1, u, half_codes[:], half_scales[:])
+
         for u in range(2):
-            cols = slice(MH * u, MH * (u + 1))
-            y = held([P, PACK, MH], F32, f"y{u}")
+            y = held([P, PACK, M_HALF], F32, f"y{u}")
             for t in range(2):
                 nc.scalar.activation(
-                    out=y[:, t, :], in_=y_acc[u][t // 2][:, t % 2, :], func=ACT.Identity, bias=bo_sb[:, t : t + 1]
+                    out=y[:, t, :], in_=y_acc[u][0][:, t, :], func=ACT.Identity, bias=bo_sb[:, t : t + 1]
                 )
             nc.vector.tensor_tensor(
-                out=y[:, 2:4, :],
+                out=y[:, 2:PACK, :],
                 in0=y_acc[u][1][:],
-                in1=bo_sb[:, 2:4].unsqueeze(2).to_broadcast([P, 2, MH]),
+                in1=bo_sb[:, 2:PACK].unsqueeze(2).to_broadcast([P, 2, M_HALF]),
                 op=ALU.add,
             )
-            nc.sync.dma_start(out=y_rows[:, :, cols], in_=y[:])
+            nc.sync.dma_start(out=y_rows[:, :, halves[u]], in_=y[:])
             nc.vector.quantize_mx(
-                out=y_codes[:, cols].bitcast(FP8X4), scales=y_scales[:, cols], in_=weave([nc.vector.tensor_copy,nc.vector.tensor_copy][u], y[:], MH)
+                out=y_codes[:, halves[u]].bitcast(FP8X4),
+                scales=y_scales[:, halves[u]],
+                in_=weave(nc.vector.tensor_copy, y[:], M_HALF),
             )
-            nc.sync.dma_start(out=y_words[:, cols], in_=y_codes[:, cols].bitcast(I32))
-        for q in range(4):
+            nc.sync.dma_start(out=y_words[:, halves[u]], in_=y_codes[:, halves[u]].bitcast(I32))
+        for q in quadrants:
             queue = nc.scalar if q % 2 == 0 else nc.sync
             queue.dma_start(
-                out=out_2[0].bitcast(I32)[4 * q : 4 * q + 4, :], in_=y_scales[32 * q : 32 * q + 4, :].bitcast(I32)
+                out=out_2[0].bitcast(I32)[SCALE_ROWS * q : SCALE_ROWS * (q + 1), :],
+                in_=y_scales[QUADRANT * q : QUADRANT * q + SCALE_ROWS, :].bitcast(I32),
             )

@@ -27,6 +27,7 @@ CHUNK = HALF // PACK
 M_HALF = M // 2
 LINE = 4
 SCALAR_SHARE = 96
+GPSIMD_ROW_SETS = 6
 STAGED_BUFS = 6
 FLOPS = 2 * K * H * S + 2 * H * H * S + 2 * H * N * M
 
@@ -78,17 +79,19 @@ def tile_list_tremolo_evenness_adviser_kernel(
         quadrants = range(P // QUADRANT)
         nc.sync.dma_start(list1[:], offs)
         nc.sync.dma_start(out=w2_w_raw[:].bitcast(I32), in_=w2_words.bitcast(I32).rearrange("a p c -> p a c"))
-        for q in quadrants:
+        for quad in quadrants:
             nc.sync.dma_start(
-                out=tab_s[QUADRANT * q : QUADRANT * q + PASSES * SCALE_ROWS, :].bitcast(I32),
-                in_=tab_scales.bitcast(I32)[:, SCALE_ROWS * q : SCALE_ROWS * (q + 1), :],
+                out=tab_s[QUADRANT * quad : QUADRANT * quad + PASSES * SCALE_ROWS, :].bitcast(I32),
+                in_=tab_scales.bitcast(I32)[:, SCALE_ROWS * quad : SCALE_ROWS * (quad + 1), :],
             )
         load_tab(0)
         load_w1(0, 0)
-        for q in quadrants:
+        for quad in quadrants:
             nc.sync.dma_start(
-                out=w2_s_raw[QUADRANT * q : QUADRANT * q + SCALE_ROWS, :, :].bitcast(I32),
-                in_=w2_scales.bitcast(I32)[:, SCALE_ROWS * q : SCALE_ROWS * (q + 1), :].rearrange("a r c -> r a c"),
+                out=w2_s_raw[QUADRANT * quad : QUADRANT * quad + SCALE_ROWS, :, :].bitcast(I32),
+                in_=w2_scales.bitcast(I32)[:, SCALE_ROWS * quad : SCALE_ROWS * (quad + 1), :].rearrange(
+                    "a r c -> r a c"
+                ),
             )
         load_w1(1, 0)
         load_tab(1)
@@ -104,8 +107,8 @@ def tile_list_tremolo_evenness_adviser_kernel(
         w2_w = held([P, PASSES, 2 * H], U8, "w2_w")
         w2_s = held([P, PASSES, H], U8, "w2_s")
         nc.scalar.copy(
-            out=w2_w[:].bitcast(U16).rearrange("p a (b i m) -> p (a b) m i", b=PASSES, i=PACK),
-            in_=w2_w_raw[:].bitcast(U16).rearrange("p a (b m i) -> p (a b) m i", b=PASSES, i=PACK),
+            out=w2_w[:].bitcast(U16).rearrange("p a (b i g) -> p (a b) g i", b=PASSES, i=PACK),
+            in_=w2_w_raw[:].bitcast(U16).rearrange("p a (b g i) -> p (a b) g i", b=PASSES, i=PACK),
         )
 
         v_w = [[held([P, HALF], U32, f"v_w{a}{c}") for c in range(2)] for a in range(PASSES)]
@@ -118,18 +121,18 @@ def tile_list_tremolo_evenness_adviser_kernel(
         for c in range(2):
             gather(v_s[c], tab_s, c)
         nc.vector.tensor_copy(
-            out=w2_s[:].rearrange("p a (b i m) -> p (a b) m i", b=PASSES, i=PACK),
-            in_=w2_s_raw[:].rearrange("p a (b m i) -> p (a b) m i", b=PASSES, i=PACK),
+            out=w2_s[:].rearrange("p a (b i g) -> p (a b) g i", b=PASSES, i=PACK),
+            in_=w2_s_raw[:].rearrange("p a (b g i) -> p (a b) g i", b=PASSES, i=PACK),
         )
 
         def deal(copy, raw, rounded, lo, hi):
             copy(
-                out=rounded[:].rearrange("p t m j -> p m j t")[:, lo:hi],
-                in_=raw[:].rearrange("p j (m t) -> p m j t", t=PACK)[:, lo:hi],
+                out=rounded[:].rearrange("p t g j -> p g j t")[:, lo:hi],
+                in_=raw[:].rearrange("p j (g t) -> p g j t", t=PACK)[:, lo:hi],
             )
 
-        def quantize(values, name, width):
-            codes = held([P, width], U32, name + "_c")
+        def quantize(values, name, width, codes_in=None):
+            codes = held([P, width], U32, codes_in or name + "_c")
             scales = held([P, width], U8, name + "_s")
             nc.vector.quantize_mx(out=codes[:].bitcast(FP8X4), scales=scales[:], in_=values)
             return codes, scales
@@ -142,7 +145,7 @@ def tile_list_tremolo_evenness_adviser_kernel(
                 deal(nc.scalar.copy, w1_raw[a, b], rounded, 0, scalar_groups)
             if scalar_groups < P:
                 deal(nc.vector.tensor_copy, w1_raw[a, b], rounded, scalar_groups, P)
-            w1_q[a, b] = quantize(rounded[:].rearrange("p t m j -> p (t m j)"), f"w1q{a}{b}", PASS)
+            w1_q[a, b] = quantize(rounded[:].rearrange("p t g j -> p (t g j)"), f"w1q{a}{b}", PASS)
 
         for c in range(2):
             gather(v_w[0][c], tab_w[0], c)
@@ -162,21 +165,21 @@ def tile_list_tremolo_evenness_adviser_kernel(
         x_banks = {}
         x_kept = {}
 
-        def weave(copy, rows, width):
+        def weave(rows, width):
             woven = woven_tile(width)
-            copy(
-                out=woven[:].rearrange("p (c q) t -> p c t q", q=LINE),
-                in_=rows.rearrange("p t (c q) -> p c t q", q=LINE),
+            nc.vector.tensor_copy(
+                out=woven[:].rearrange("p (c e) t -> p c t e", e=LINE),
+                in_=rows.rearrange("p t (c e) -> p c t e", e=LINE),
             )
             return woven[:].rearrange("p c t -> p (c t)")
 
         def first_stage(b, c, banks, f, engine, pieces):
             gelu = ring.tile([P, HALF, PACK], F32, name="gelu", align_bytes=64)
             x_banks[b, c] = []
-            for n in range(HALF // CHUNK):
-                acc = psum.tile([P, PACK, CHUNK], F32, name=f"{banks}{n}")
+            for bank in range(HALF // CHUNK):
+                acc = psum.tile([P, PACK, CHUNK], F32, name=f"{banks}{bank}")
                 x_banks[b, c].append(acc)
-                cols = slice(CHUNK * n, CHUNK * (n + 1))
+                cols = slice(CHUNK * bank, CHUNK * (bank + 1))
                 for i in range(PACK):
                     for a in range(PASSES):
                         codes, scales = w1_q[a, b]
@@ -204,8 +207,8 @@ def tile_list_tremolo_evenness_adviser_kernel(
 
         def keep_x(b, c, kept):
             x_kept[b, c] = kept
-            for n in range(HALF // CHUNK):
-                nc.scalar.copy(out=kept[:, n], in_=x_banks[b, c][n][:])
+            for bank in range(HALF // CHUNK):
+                nc.scalar.copy(out=kept[:, bank], in_=x_banks[b, c][bank][:])
 
         def second_stage(b, i, c):
             cols = slice(HALF * c, HALF * (c + 1))
@@ -223,8 +226,8 @@ def tile_list_tremolo_evenness_adviser_kernel(
                     stop=(a == PASSES - 1),
                 )
             nc.vector.tensor_tensor(
-                out=h[b][i][:, cols].rearrange("p (n j) -> p n j", j=CHUNK),
-                in0=acc[:].rearrange("p (n j) -> p n j", j=CHUNK),
+                out=h[b][i][:, cols].rearrange("p (run j) -> p run j", j=CHUNK),
+                in0=acc[:].rearrange("p (run j) -> p run j", j=CHUNK),
                 in1=x_kept[b, c][:, :, i, :],
                 op=ALU.max,
             )
@@ -232,10 +235,10 @@ def tile_list_tremolo_evenness_adviser_kernel(
 
         w3_q = {}
 
-        def prepare_w3(b):
+        def prepare_w3(b, codes_in=None):
             rounded = held([P, PACK, P, PACK], BF16, f"rounded{b}")
             deal(nc.scalar.copy, w3_raw[b], rounded, 0, P)
-            w3_q[b] = quantize(rounded[:].rearrange("p t m j -> p (t m j)"), f"w3q{b}", N)
+            w3_q[b] = quantize(rounded[:].rearrange("p t g j -> p (t g j)"), f"w3q{b}", N, codes_in)
 
         x_shape = [P, HALF // CHUNK, PACK, CHUNK]
         f_late = held([P, PASSES, HALF, PACK], BF16, "f_late")
@@ -257,8 +260,7 @@ def tile_list_tremolo_evenness_adviser_kernel(
         late_codes, late_scales = quantize(f_late[:].rearrange("p b c t -> p (b c t)"), "fq_late", PASSES * HALF)
         for a in range(PASSES):
             f_q[a, 1] = (late_codes[:, HALF * a : HALF * (a + 1)], late_scales[:, HALF * a : HALF * (a + 1)])
-        for b in range(PASSES):
-            prepare_w3(b)
+        prepare_w3(0)
 
         neg_top = {}
 
@@ -273,18 +275,24 @@ def tile_list_tremolo_evenness_adviser_kernel(
             nc.scalar.activation(out=seen[:], in_=h[b][i][:].indirect(entries), func=ACT.Exp, bias=neg_top[b, i][:])
             return seen
 
-        def weigh(seen, b, i, lo, hi, d_rows):
-            nc.vector.scalar_tensor_tensor(
-                out=d_rows[:, i, :],
-                in0=seen[:],
-                scalar=tilt_sb[:, b, i : i + 1],
-                in1=mat_sb[b][:, i, lo:hi],
-                op0=ALU.add,
-                op1=ALU.mult,
-            )
+        def lift(seen, b, i, lifted):
+            column = tilt_sb[:, b, i : i + 1]
+            if PACK * b + i < GPSIMD_ROW_SETS:
+                nc.gpsimd.tensor_scalar(
+                    out=lifted[:, i, :], in0=seen[:], scalar1=column, scalar2=1.0, op0=ALU.add, op1=ALU.mult
+                )
+            else:
+                nc.scalar.activation(out=lifted[:, i, :], in_=seen[:], func=ACT.Identity, bias=column)
 
-        def d_tile(width):
-            return ring.tile([P, PACK, width], BF16, name="d_rows", bufs=3, align_bytes=64)
+        def weigh(lifted, b, lo, hi):
+            woven = woven_tile(hi - lo)
+            nc.vector.tensor_tensor(
+                out=woven[:].rearrange("p (c e) t -> p c t e", e=LINE),
+                in0=lifted.rearrange("p t (c e) -> p c t e", e=LINE),
+                in1=mat_sb[b][:, :, lo:hi].rearrange("p t (c e) -> p c t e", e=LINE),
+                op=ALU.mult,
+            )
+            return woven[:].rearrange("p c t -> p (c t)")
 
         y_acc = [[psum.tile([P, 2, M_HALF], F32, name=f"high{2 * u + s}") for s in range(2)] for u in range(2)]
 
@@ -301,30 +309,29 @@ def tile_list_tremolo_evenness_adviser_kernel(
                     stop=(b == PASSES - 1 and t % 2 == 1),
                 )
 
-        d_first = d_tile(M)
-        seen_first = []
+        lifted_first = held([P, PACK, M], F32, "lifted_first")
         for i in range(PACK):
             close_rows(0, i)
-            seen_first.append(look(0, i, 0, M))
+            lift(look(0, i, 0, M), 0, i, lifted_first)
         for i in range(PACK):
             close_rows(1, i)
-        for i in range(PACK):
-            weigh(seen_first[i], 0, i, 0, M, d_first)
-        d_codes, d_scales = quantize(weave(nc.scalar.copy, d_first[:], M), "dq0", M)
+        prepare_w3(1, "fq_late_c")
         halves = [slice(M_HALF * u, M_HALF * (u + 1)) for u in range(2)]
         for u in range(2):
-            third_stage(0, u, d_codes[:, halves[u]], d_scales[:, halves[u]])
+            lo, hi = halves[u].start, halves[u].stop
+            d_codes, d_scales = quantize(weigh(lifted_first[:, :, lo:hi], 0, lo, hi), f"dq0{u}", M_HALF)
+            third_stage(0, u, d_codes[:], d_scales[:])
 
         y_rows = out_0.rearrange("(p t) m -> p t m", t=PACK)
         y_codes = held([P, M], U32, "y_codes")
         y_scales = held([P, M], U8, "y_scales")
         y_words = out_1[0].rearrange("p m t -> p (m t)").bitcast(I32)
         for u in range(2):
-            d_half = d_tile(M_HALF)
+            lifted = held([P, PACK, M_HALF], F32, f"lifted{u}")
             lo, hi = halves[u].start, halves[u].stop
             for i in range(PACK):
-                weigh(look(1, i, lo, hi), 1, i, lo, hi, d_half)
-            half_codes, half_scales = quantize(weave(nc.vector.tensor_copy, d_half[:], M_HALF), f"dq1{u}", M_HALF)
+                lift(look(1, i, lo, hi), 1, i, lifted)
+            half_codes, half_scales = quantize(weigh(lifted[:], 1, lo, hi), f"dq1{u}", M_HALF)
             third_stage(1, u, half_codes[:], half_scales[:])
 
         for u in range(2):
@@ -343,12 +350,12 @@ def tile_list_tremolo_evenness_adviser_kernel(
             nc.vector.quantize_mx(
                 out=y_codes[:, halves[u]].bitcast(FP8X4),
                 scales=y_scales[:, halves[u]],
-                in_=weave(nc.vector.tensor_copy, y[:], M_HALF),
+                in_=weave(y[:], M_HALF),
             )
             nc.sync.dma_start(out=y_words[:, halves[u]], in_=y_codes[:, halves[u]].bitcast(I32))
-        for q in quadrants:
-            queue = nc.scalar if q % 2 == 0 else nc.sync
+        for quad in quadrants:
+            queue = nc.scalar if quad % 2 == 0 else nc.sync
             queue.dma_start(
-                out=out_2[0].bitcast(I32)[SCALE_ROWS * q : SCALE_ROWS * (q + 1), :],
-                in_=y_scales[QUADRANT * q : QUADRANT * q + SCALE_ROWS, :].bitcast(I32),
+                out=out_2[0].bitcast(I32)[SCALE_ROWS * quad : SCALE_ROWS * (quad + 1), :],
+                in_=y_scales[QUADRANT * quad : QUADRANT * quad + SCALE_ROWS, :].bitcast(I32),
             )

from contextlib import ExitStack

import concourse.mybir as mybir

F32 = mybir.dt.float32
BF16 = mybir.dt.bfloat16
I32 = mybir.dt.int32
U32 = mybir.dt.uint32
U16 = mybir.dt.uint16
U8 = mybir.dt.uint8
FP8X4 = mybir.dt.float8_e4m3fn_x4
FP4X4 = mybir.dt.float4_e2m1fn_x4
ACT = mybir.ActivationFunctionType
ALU = mybir.AluOpType
AX = mybir.AxisListType

K, H, N, T, S, M = 1024, 1024, 512, 2048, 1024, 512
P = 128
PACK = 4
PASS = P * PACK
PASSES = 2
STRIPE = 16
QUADRANT = 32
SCALE_ROWS = 4
HALF = S // 2
CHUNK = HALF // PACK
M_HALF = M // 2
LINE = 4
SCALAR_SHARE = 96
GPSIMD_ROW_SETS = 6
STAGED_BUFS = 6
FLOPS = 2 * K * H * S + 2 * H * H * S + 2 * H * N * M


def tile_list_tremolo_evenness_adviser_kernel(
    tc, tab_words, tab_scales, offs, w1, gain, w2_words, w2_scales, offs2, tilt, mat, w3, bo, out_0, out_1, out_2
):
    nc = tc.nc
    with ExitStack() as ctx:
        keep = ctx.enter_context(tc.tile_pool(name="keep", bufs=1))
        ring = ctx.enter_context(tc.tile_pool(name="ring", bufs=2))
        psum = ctx.enter_context(tc.psum_pool(name="psum", bufs=1))

        def held(shape, dtype, name):
            return keep.tile(shape, dtype, name=name, align_bytes=64)

        def staged(shape):
            return ring.tile(shape, F32, name="staged", bufs=STAGED_BUFS, align_bytes=64)

        def woven_tile(width):
            return ring.tile([P, width, PACK], BF16, name="woven", bufs=3, align_bytes=64)

        def load_rows(tile, rows):
            nc.sync.dma_start(out=tile[:], in_=rows.rearrange("(p j) c -> p j c", j=PACK))

        list1 = keep.tile([P, S // STRIPE], U16, name="list1")
        list2 = keep.tile([P, M // STRIPE], U16, name="list2")
        tab_w = [held([P, T], U32, f"big{a}") for a in range(PASSES)]
        tab_s = held([P, T], U8, "tab_s")
        w2_w_raw = held([P, PASSES, 2 * H], U8, "w2_w_raw")
        w2_s_raw = held([P, PASSES, H], U8, "w2_s_raw")
        w1_raw = {(a, b): staged([P, PACK, PASS]) for b in range(PASSES) for a in range(PASSES)}
        w3_raw = [staged([P, PACK, N]) for b in range(PASSES)]
        gain_sb = held([P, PASSES, PACK], F32, "gain_sb")
        tilt_sb = held([P, PASSES, PACK], F32, "tilt_sb")
        bo_sb = held([P, PACK], F32, "bo_sb")

        nc.vector.memset(tab_s[:].bitcast(I32), 0)
        nc.vector.memset(w2_s_raw[:].bitcast(I32), 0)

        def load_w1(a, b):
            load_rows(w1_raw[a, b], w1[PASS * a : PASS * (a + 1), PASS * b : PASS * (b + 1)])

        def load_tab(a):
            nc.sync.dma_start(
                out=tab_w[a][:].bitcast(I32), in_=tab_words[a].rearrange("p t i -> p (t i)").bitcast(I32)
            )

        quadrants = range(P // QUADRANT)
        nc.sync.dma_start(list1[:], offs)
        nc.sync.dma_start(out=w2_w_raw[:].bitcast(I32), in_=w2_words.bitcast(I32).rearrange("a p c -> p a c"))
        for quad in quadrants:
            nc.sync.dma_start(
                out=tab_s[QUADRANT * quad : QUADRANT * quad + PASSES * SCALE_ROWS, :].bitcast(I32),
                in_=tab_scales.bitcast(I32)[:, SCALE_ROWS * quad : SCALE_ROWS * (quad + 1), :],
            )
        load_tab(0)
        load_w1(0, 0)
        for quad in quadrants:
            nc.sync.dma_start(
                out=w2_s_raw[QUADRANT * quad : QUADRANT * quad + SCALE_ROWS, :, :].bitcast(I32),
                in_=w2_scales.bitcast(I32)[:, SCALE_ROWS * quad : SCALE_ROWS * (quad + 1), :].rearrange(
                    "a r c -> r a c"
                ),
            )
        load_w1(1, 0)
        load_tab(1)
        load_w1(0, 1)
        load_w1(1, 1)
        nc.sync.dma_start(out=gain_sb[:], in_=gain.rearrange("(b p i) -> p b i", b=PASSES, i=PACK))
        nc.sync.dma_start(list2[:], offs2)
        nc.sync.dma_start(out=tilt_sb[:], in_=tilt.rearrange("(b p i) -> p b i", b=PASSES, i=PACK))
        nc.sync.dma_start(out=bo_sb[:], in_=bo.rearrange("(p i) -> p i", i=PACK))
        for b in range(PASSES):
            load_rows(w3_raw[b], w3[PASS * b : PASS * (b + 1), :])

        w2_w = held([P, PASSES, 2 * H], U8, "w2_w")
        w2_s = held([P, PASSES, H], U8, "w2_s")
        nc.scalar.copy(
            out=w2_w[:].bitcast(U16).rearrange("p a (b i g) -> p (a b) g i", b=PASSES, i=PACK),
            in_=w2_w_raw[:].bitcast(U16).rearrange("p a (b g i) -> p (a b) g i", b=PASSES, i=PACK),
        )

        v_w = [[held([P, HALF], U32, f"v_w{a}{c}") for c in range(2)] for a in range(PASSES)]
        v_s = [held([P, HALF], U8, f"v_s{c}") for c in range(2)]

        def gather(out, window, c):
            entries = list1[:, HALF // STRIPE * c : HALF // STRIPE * (c + 1)]
            nc.vector.tensor_copy(out=out[:], in_=window[:].indirect(entries))

        for c in range(2):
            gather(v_s[c], tab_s, c)
        nc.vector.tensor_copy(
            out=w2_s[:].rearrange("p a (b i g) -> p (a b) g i", b=PASSES, i=PACK),
            in_=w2_s_raw[:].rearrange("p a (b g i) -> p (a b) g i", b=PASSES, i=PACK),
        )

        def deal(copy, raw, rounded, lo, hi):
            copy(
                out=rounded[:].rearrange("p t g j -> p g j t")[:, lo:hi],
                in_=raw[:].rearrange("p j (g t) -> p g j t", t=PACK)[:, lo:hi],
            )

        def quantize(values, name, width, codes_in=None):
            codes = held([P, width], U32, codes_in or name + "_c")
            scales = held([P, width], U8, name + "_s")
            nc.vector.quantize_mx(out=codes[:].bitcast(FP8X4), scales=scales[:], in_=values)
            return codes, scales

        w1_q = {}

        def prepare_w1(a, b, scalar_groups):
            rounded = held([P, PACK, P, PACK], BF16, f"rounded{a}")
            if scalar_groups > 0:
                deal(nc.scalar.copy, w1_raw[a, b], rounded, 0, scalar_groups)
            if scalar_groups < P:
                deal(nc.vector.tensor_copy, w1_raw[a, b], rounded, scalar_groups, P)
            w1_q[a, b] = quantize(rounded[:].rearrange("p t g j -> p (t g j)"), f"w1q{a}{b}", PASS)

        for c in range(2):
            gather(v_w[0][c], tab_w[0], c)
        prepare_w1(0, 0, P)
        prepare_w1(1, 0, SCALAR_SHARE)
        for c in range(2):
            gather(v_w[1][c], tab_w[1], c)
        prepare_w1(0, 1, 0)
        prepare_w1(1, 1, 0)

        mat_sb = [staged([P, PACK, M]) for b in range(PASSES)]
        for b in range(PASSES):
            load_rows(mat_sb[b], mat[PASS * b : PASS * (b + 1), :])
        h = [[held([P, S], F32, f"h{b}{i}") for i in range(PACK)] for b in range(PASSES)]
        half_top = [[held([P, 2], F32, f"half_top{b}{i}") for i in range(PACK)] for b in range(PASSES)]
        f_q = {}
        x_banks = {}
        x_kept = {}

        def weave(rows, width):
            woven = woven_tile(width)
            nc.vector.tensor_copy(
                out=woven[:].rearrange("p (c e) t -> p c t e", e=LINE),
                in_=rows.rearrange("p t (c e) -> p c t e", e=LINE),
            )
            return woven[:].rearrange("p c t -> p (c t)")

        def first_stage(b, c, banks, f, engine, pieces):
            gelu = ring.tile([P, HALF, PACK], F32, name="gelu", align_bytes=64)
            x_banks[b, c] = []
            for bank in range(HALF // CHUNK):
                acc = psum.tile([P, PACK, CHUNK], F32, name=f"{banks}{bank}")
                x_banks[b, c].append(acc)
                cols = slice(CHUNK * bank, CHUNK * (bank + 1))
                for i in range(PACK):
                    for a in range(PASSES):
                        codes, scales = w1_q[a, b]
                        nc.tensor.matmul_mx(
                            out=acc[:, i, :],
                            lhsT=codes[:, P * i : P * (i + 1)].bitcast(FP8X4),
                            lhsT_scale=scales[:, P * i : P * (i + 1)],
                            rhs=v_w[a][c][:, cols].bitcast(FP8X4),
                            rhs_scale=v_s[c][SCALE_ROWS * a : P, cols],
                            start=(a == 0),
                            stop=(a == PASSES - 1),
                        )
                nc.scalar.activation(
                    out=gelu[:, cols, :], in_=acc[:].rearrange("p i j -> p j i"), func=ACT.Gelu_apprx_tanh
                )
            width = HALF // pieces
            for piece in range(pieces):
                cols = slice(width * piece, width * (piece + 1))
                engine.tensor_tensor(
                    out=f[:, cols, :],
                    in0=gelu[:, cols, :],
                    in1=gain_sb[:, b, :].unsqueeze(1).to_broadcast([P, width, PACK]),
                    op=ALU.mult,
                )

        def keep_x(b, c, kept):
            x_kept[b, c] = kept
            for bank in range(HALF // CHUNK):
                nc.scalar.copy(out=kept[:, bank], in_=x_banks[b, c][bank][:])

        def second_stage(b, i, c):
            cols = slice(HALF * c, HALF * (c + 1))
            acc = psum.tile([P, HALF], F32, name=f"low{2 * c + i % 2}")
            first = PASS * b + P * i
            for a in range(PASSES):
                codes, scales = f_q[a, c]
                nc.tensor.matmul_mx(
                    out=acc[:],
                    lhsT=w2_w[:, a, 2 * first : 2 * (first + P)].bitcast(FP4X4),
                    lhsT_scale=w2_s[:, a, first : first + P],
                    rhs=codes[:].bitcast(FP8X4),
                    rhs_scale=scales[:],
                    start=(a == 0),
                    stop=(a == PASSES - 1),
                )
            nc.vector.tensor_tensor(
                out=h[b][i][:, cols].rearrange("p (run j) -> p run j", j=CHUNK),
                in0=acc[:].rearrange("p (run j) -> p run j", j=CHUNK),
                in1=x_kept[b, c][:, :, i, :],
                op=ALU.max,
            )
            nc.vector.tensor_reduce(out=half_top[b][i][:, c : c + 1], in_=h[b][i][:, cols], axis=AX.X, op=ALU.max)

        w3_q = {}

        def prepare_w3(b, codes_in=None):
            rounded = held([P, PACK, P, PACK], BF16, f"rounded{b}")
            deal(nc.scalar.copy, w3_raw[b], rounded, 0, P)
            w3_q[b] = quantize(rounded[:].rearrange("p t g j -> p (t g j)"), f"w3q{b}", N, codes_in)

        x_shape = [P, HALF // CHUNK, PACK, CHUNK]
        f_late = held([P, PASSES, HALF, PACK], BF16, "f_late")
        x_early = []
        for b in range(PASSES):
            f = held([P, HALF, PACK], BF16, "rounded1") if b == 0 else woven_tile(HALF)
            x_early.append(held(x_shape, F32, f"big{b}"))
            first_stage(b, 0, ("low", "high")[b], f[:], nc.vector, 1)
            f_q[b, 0] = quantize(f[:].rearrange("p c t -> p (c t)"), f"fq{b}0", HALF)
        for b in range(PASSES):
            keep_x(b, 0, x_early[b])
        for b in range(PASSES):
            kept = staged(x_shape)
            first_stage(b, 1, "high", f_late[:, b], nc.gpsimd, HALF // CHUNK)
            keep_x(b, 1, kept)
        for b in range(PASSES):
            for i in range(PACK):
                second_stage(b, i, 0)
        late_codes, late_scales = quantize(f_late[:].rearrange("p b c t -> p (b c t)"), "fq_late", PASSES * HALF)
        for a in range(PASSES):
            f_q[a, 1] = (late_codes[:, HALF * a : HALF * (a + 1)], late_scales[:, HALF * a : HALF * (a + 1)])
        prepare_w3(0)

        neg_top = {}

        def close_rows(b, i):
            neg_top[b, i] = held([P, 1], F32, f"neg_top{b}{i}")
            second_stage(b, i, 1)
            nc.vector.tensor_reduce(out=neg_top[b, i][:], in_=half_top[b][i][:], axis=AX.X, op=ALU.max, negate=True)

        def look(b, i, lo, hi):
            seen = held([P, hi - lo], F32, f"seen{b}{i}{lo}")
            entries = list2[:, lo // STRIPE : hi // STRIPE]
            nc.scalar.activation(out=seen[:], in_=h[b][i][:].indirect(entries), func=ACT.Exp, bias=neg_top[b, i][:])
            return seen

        def lift(seen, b, i, lifted):
            column = tilt_sb[:, b, i : i + 1]
            if PACK * b + i < GPSIMD_ROW_SETS:
                nc.gpsimd.tensor_scalar(
                    out=lifted[:, i, :], in0=seen[:], scalar1=column, scalar2=1.0, op0=ALU.add, op1=ALU.mult
                )
            else:
                nc.scalar.activation(out=lifted[:, i, :], in_=seen[:], func=ACT.Identity, bias=column)

        def weigh(lifted, b, lo, hi):
            woven = woven_tile(hi - lo)
            nc.vector.tensor_tensor(
                out=woven[:].rearrange("p (c e) t -> p c t e", e=LINE),
                in0=lifted.rearrange("p t (c e) -> p c t e", e=LINE),
                in1=mat_sb[b][:, :, lo:hi].rearrange("p t (c e) -> p c t e", e=LINE),
                op=ALU.mult,
            )
            return woven[:].rearrange("p c t -> p (c t)")

        y_acc = [[psum.tile([P, 2, M_HALF], F32, name=f"high{2 * u + s}") for s in range(2)] for u in range(2)]

        def third_stage(b, u, codes, scales):
            w_codes, w_scales = w3_q[b]
            for t in range(PACK):
                nc.tensor.matmul_mx(
                    out=y_acc[u][t // 2][:, t % 2, :],
                    lhsT=w_codes[:, P * t : P * (t + 1)].bitcast(FP8X4),
                    lhsT_scale=w_scales[:, P * t : P * (t + 1)],
                    rhs=codes.bitcast(FP8X4),
                    rhs_scale=scales,
                    start=(b == 0 and t % 2 == 0),
                    stop=(b == PASSES - 1 and t % 2 == 1),
                )

        lifted_first = held([P, PACK, M], F32, "lifted_first")
        for i in range(PACK):
            close_rows(0, i)
            lift(look(0, i, 0, M), 0, i, lifted_first)
        for i in range(PACK):
            close_rows(1, i)
        prepare_w3(1, "fq_late_c")
        halves = [slice(M_HALF * u, M_HALF * (u + 1)) for u in range(2)]
        for u in range(2):
            lo, hi = halves[u].start, halves[u].stop
            d_codes, d_scales = quantize(weigh(lifted_first[:, :, lo:hi], 0, lo, hi), f"dq0{u}", M_HALF)
            third_stage(0, u, d_codes[:], d_scales[:])

        y_rows = out_0.rearrange("(p t) m -> p t m", t=PACK)
        y_codes = held([P, M], U32, "y_codes")
        y_scales = held([P, M], U8, "y_scales")
        y_words = out_1[0].rearrange("p m t -> p (m t)").bitcast(I32)
        for u in range(2):
            lifted = held([P, PACK, M_HALF], F32, f"lifted{u}")
            lo, hi = halves[u].start, halves[u].stop
            for i in range(PACK):
                lift(look(1, i, lo, hi), 1, i, lifted)
            half_codes, half_scales = quantize(weigh(lifted[:], 1, lo, hi), f"dq1{u}", M_HALF)
            third_stage(1, u, half_codes[:], half_scales[:])

        for u in range(2):
            y = held([P, PACK, M_HALF], F32, f"y{u}")
            for t in range(2):
                nc.scalar.activation(
                    out=y[:, t, :], in_=y_acc[u][0][:, t, :], func=ACT.Identity, bias=bo_sb[:, t : t + 1]
                )
            nc.vector.tensor_tensor(
                out=y[:, 2:PACK, :],
                in0=y_acc[u][1][:],
                in1=bo_sb[:, 2:PACK].unsqueeze(2).to_broadcast([P, 2, M_HALF]),
                op=ALU.add,
            )
            nc.sync.dma_start(out=y_rows[:, :, halves[u]], in_=y[:])
            nc.vector.quantize_mx(
                out=y_codes[:, halves[u]].bitcast(FP8X4),
                scales=y_scales[:, halves[u]],
                in_=weave(y[:], M_HALF),
            )
            nc.sync.dma_start(out=y_words[:, halves[u]], in_=y_codes[:, halves[u]].bitcast(I32))
        for quad in quadrants:
            queue = nc.scalar if quad % 2 == 0 else nc.sync
            queue.dma_start(
                out=out_2[0].bitcast(I32)[SCALE_ROWS * quad : SCALE_ROWS * (quad + 1), :],
                in_=y_scales[QUADRANT * quad : QUADRANT * quad + SCALE_ROWS, :].bitcast(I32),
            )
